import numpy as np
import ml_dtypes


def mxq(x, axis, fmt="e4m3"):
    dtype, down = {"e4m3": (ml_dtypes.float8_e4m3fn, 7), "e5m2": (ml_dtypes.float8_e5m2, 14)}[fmt]
    v = np.moveaxis(np.asarray(x, np.float32).astype(ml_dtypes.bfloat16).astype(np.float64), axis, -1)
    blocks = v.reshape(v.shape[:-1] + (-1, 32))
    amax = np.abs(blocks).max(-1, keepdims=True)
    byte = np.maximum(np.where(amax > 0, np.frexp(amax)[1] - 1 + 127, 0) - down, 1)
    scale = np.exp2(byte - 127.0)
    codes = (blocks / scale).astype(np.float32).astype(dtype).astype(np.float64)
    return np.moveaxis((codes * scale).reshape(v.shape), -1, axis)


WIDE = False


def mx_kscale(k):
    if not WIDE:
        return np.ones(k)
    levels = np.array([10, -10, 5, -5, 0])
    if k % 512:
        return np.exp2(np.random.permutation(np.resize(levels, k // 32))).repeat(32)
    a = np.empty((k // 512, 16))
    for p in range(k // 512):
        a[p, :8] = np.random.permutation(np.resize(levels, 8))
        for g in range(8):
            far = levels[np.abs(levels - a[p, g]) >= 10]
            a[p, g + 8] = far[np.random.randint(len(far))]
    return np.exp2(a.ravel()).repeat(32)


def f64(x):
    return np.asarray(x).astype(np.float64)


def striped(idx):
    return np.tile(idx.reshape(-1, 16).T, (8, 1)).astype(np.uint16)


def unstriped(offs):
    return offs[:16].T.reshape(-1).astype(np.int64)


E2M1 = np.array([0.0, 0.5, 1.0, 1.5, 2.0, 3.0, 4.0, 6.0, -0.0, -0.5, -1.0, -1.5, -2.0, -3.0, -4.0, -6.0])


def pack_weight(w, fmt):
    k, n = w.shape
    w = f64(np.asarray(w, np.float32).astype(ml_dtypes.bfloat16)).reshape(k // 32, 32, n)
    amax = np.abs(w).max(1)
    if fmt == "e4m3":
        byte = np.frexp(amax)[1] - 1 + 127 - 7
    else:
        mant, ex = np.frexp(amax / 6.0)
        byte = np.where(mant > 0.5, ex, ex - 1) + 127
    byte = np.clip(np.where(amax > 0, byte, 1), 1, 254)
    scaled = (w * np.exp2(127.0 - byte)[:, None, :]).reshape(k, n).astype(np.float32)
    by_word = np.ascontiguousarray(scaled.reshape(k // 512, 128, 4, n).transpose(0, 1, 3, 2))
    if fmt == "e4m3":
        words = by_word.astype(ml_dtypes.float8_e4m3fn).view(np.uint8)
    else:
        c = by_word.astype(ml_dtypes.float4_e2m1fn).view(np.uint8) & 0xF
        words = (c[..., 0::2] | (c[..., 1::2] << 4)).reshape(k // 512, 128, 2 * n)
    return np.ascontiguousarray(words), np.ascontiguousarray(byte.astype(np.uint8).reshape(k // 512, 16, n))


def unpack_weight(words, scales, fmt):
    g, _, n = scales.shape
    words = np.ascontiguousarray(words).reshape(g, 128, n, -1)
    if fmt == "e4m3":
        vals = words.view(ml_dtypes.float8_e4m3fn).astype(np.float64)
    else:
        nib = np.empty((g, 128, n, 4), np.uint8)
        nib[..., 0::2] = words & 0xF
        nib[..., 1::2] = words >> 4
        vals = E2M1[nib]
    vals = vals * np.repeat(np.exp2(scales.astype(np.float64) - 127.0), 8, axis=1)[..., None]
    return vals.transpose(0, 1, 3, 2).reshape(g * 512, n)


K, M, T, S = 1536, 1024, 2048, 1024


def setup_inputs():
    n = np.random.standard_normal
    s = mx_kscale(K)[:, None]
    u = mx_kscale(512)[:, None]
    v = pack_weight(n((K, T)) * s, "e4m3")
    p_w4 = pack_weight(n((K, M)) / np.sqrt(K) / s, "e2m1")
    return {
        "tab_words": v[0],
        "tab_scales": v[1],
        "w4_words": p_w4[0],
        "w4_scales": p_w4[1],
        "down": (n((K, 512)) / np.sqrt(K) / s * u.T).astype(np.float32),
        "up": (0.5 * n((512, M)) / np.sqrt(512) / u).astype(np.float32),
        "rT": n((M, T)).astype(np.float32),
        "b": (0.3 * n(1024)).astype(np.float32),
        "offs": striped(np.random.permutation(T)[:S]),
    }


def reference(tab_words, tab_scales, w4_words, w4_scales, down, up, rT, b, offs):
    tab_ = unpack_weight(tab_words, tab_scales, "e4m3")[:, unstriped(offs)]
    w4_ = unpack_weight(w4_words, w4_scales, "e2m1")
    down_ = mxq(f64(down), 0, "e4m3")
    up_ = mxq(f64(up), 0, "e4m3")
    h_ = mxq(down_.T @ tab_, 0, "e4m3")
    y = w4_.T @ tab_ + up_.T @ h_
    return (y + f64(b)[:, None]) + f64(rT)[:, unstriped(offs)]

@@ -1,0 +1,218 @@
+from contextlib import ExitStack
+
+import concourse.mybir as mybir
+from concourse.masks import make_identity
+
+K, M, T, S, R = 1536, 1024, 2048, 1024, 512
+FLOPS = 2 * S * (K * R + K * M + R * M)
+
+F32 = mybir.dt.float32
+BF16 = mybir.dt.bfloat16
+I32 = mybir.dt.int32
+U32 = mybir.dt.uint32
+U16 = mybir.dt.uint16
+U8 = mybir.dt.uint8
+FP8X4 = mybir.dt.float8_e4m3fn_x4
+FP4X4 = mybir.dt.float4_e2m1fn_x4
+ADD = mybir.AluOpType.add
+
+P = 128
+PACK = 4
+K_PASS = P * PACK
+PASSES = K // K_PASS
+BANK = 512
+HALVES = S // BANK
+ROW_TILES = M // P
+H_COLS = BANK // PACK
+LIST_ROWS = 16
+
+
+def tile_list_tabres_bias_kernel(
+    tc, tab_words, tab_scales, w4_words, w4_scales, down, up, rT, b, offs, out
+):
+    nc = tc.nc
+    with ExitStack() as ctx:
+        keep = ctx.enter_context(tc.tile_pool(name="keep", bufs=1))
+        resid = ctx.enter_context(tc.tile_pool(name="resid", bufs=7))
+        h_psum = ctx.enter_context(tc.psum_pool(name="h_psum", bufs=3))
+        y_psum = ctx.enter_context(tc.psum_pool(name="y_psum", bufs=5))
+
+        offsets = keep.tile([P, S // LIST_ROWS], U16, name="offsets")
+        nc.sync.dma_start(offsets[:], offs)
+
+        def list_part(first, count):
+            return offsets[:, first // LIST_ROWS : (first + count) // LIST_ROWS]
+
+        w4_scale = keep.tile([P, PASSES, M // 4], I32, name="w4_scale", align_bytes=64)
+        tab_scale = keep.tile([P, PASSES, T // 4], I32, name="tab_scale", align_bytes=64)
+        nc.vector.memset(tab_scale[:], 0)
+        nc.gpsimd.memset(w4_scale[:], 0)
+        b_rows = keep.tile([P, P], F32, name="b_rows")
+        nc.vector.memset(b_rows[:], 0.0)
+
+        def load_scales(queue, plane, source):
+            for q in range(4):
+                queue.dma_start(
+                    out=plane[32 * q : 32 * q + 4, :, :],
+                    in_=source[:, 4 * q : 4 * q + 4, :].bitcast(I32).rearrange("a r n -> r a n"),
+                )
+
+        load_scales(nc.sync, tab_scale, tab_scales)
+        load_scales(nc.sync, w4_scale, w4_scales)
+        nc.sync.dma_start(out=b_rows[0:ROW_TILES, :], in_=b.rearrange("(c p) -> c p", p=P))
+        identity = keep.tile([P, P], F32, name="identity")
+        make_identity(nc, identity[:])
+
+        table = [keep.tile([P, T], I32, name="table%d" % a, align_bytes=64) for a in range(PASSES)]
+        down_raw = [keep.tile([P, PACK, R], F32, name="down_raw%d" % a) for a in range(PASSES)]
+        up_raw = [keep.tile([P, PACK, BANK], F32, name="up_raw%d" % u) for u in range(2)]
+        w4 = keep.tile([P, PASSES, 2 * M], U8, name="w4", align_bytes=64)
+        r_rows = {}
+
+        def load_table(a):
+            nc.sync.dma_start(out=table[a][:], in_=tab_words[a].rearrange("p t i -> p (t i)").bitcast(I32))
+
+        def load_down(a):
+            rows = down[a * K_PASS : (a + 1) * K_PASS, :]
+            nc.sync.dma_start(out=down_raw[a][:], in_=rows.rearrange("(p j) r -> p j r", j=PACK))
+
+        def load_up(u):
+            cols = up[:, u * BANK : (u + 1) * BANK]
+            nc.sync.dma_start(out=up_raw[u][:], in_=cols.rearrange("(p j) n -> p j n", j=PACK))
+
+        def load_w4():
+            nc.sync.dma_start(out=w4[:].bitcast(I32), in_=w4_words.bitcast(I32).rearrange("a p n -> p a n"))
+
+        def load_residual(c):
+            r_rows[c] = resid.tile([P, T], F32, name="r_rows")
+            nc.sync.dma_start(out=r_rows[c][:], in_=rT[c * P : (c + 1) * P, :])
+
+        load_table(0)
+        load_down(0)
+        load_table(1)
+        load_down(1)
+        load_down(2)
+        load_up(0)
+        load_table(2)
+        load_residual(0)
+        load_w4()
+        load_residual(1)
+        load_residual(2)
+        load_up(1)
+        for c in range(3, 7):
+            load_residual(c)
+
+        bias_t = h_psum.tile([P, P], F32, name="h_bank")
+        nc.tensor.transpose(bias_t[:], b_rows[:], identity[:])
+        bias = keep.tile([P, ROW_TILES], F32, name="bias")
+        nc.scalar.copy(out=bias[:], in_=bias_t[:, 0:ROW_TILES])
+
+        v_words = [keep.tile([P, S], U32, name="v_words%d" % a, align_bytes=64) for a in range(PASSES)]
+        v_scale = [keep.tile([P, S], U8, name="v_scale%d" % a, align_bytes=64) for a in range(PASSES)]
+        down_words = keep.tile([P, PASSES, R], U32, name="down_words", align_bytes=64)
+        down_scale = keep.tile([P, PASSES, R], U8, name="down_scale", align_bytes=64)
+        for a in range(PASSES):
+            step = BANK if a == PASSES - 1 else S
+            for j0 in range(0, S, step):
+                nc.vector.tensor_copy(
+                    v_words[a][:, j0 : j0 + step], table[a][:].bitcast(U32).indirect(list_part(j0, step))
+                )
+            nc.vector.tensor_copy(v_scale[a][:], tab_scale[:, a, :].bitcast(U8).indirect(offsets[:]))
+            down_bf = keep.tile([P, PACK * R], BF16, name="down_bf%d" % a, align_bytes=64)
+            nc.scalar.copy(
+                out=down_bf[:].rearrange("p (t m j) -> p m j t", t=PACK, j=PACK),
+                in_=down_raw[a][:].rearrange("p j (m t) -> p m j t", t=PACK),
+            )
+            nc.vector.quantize_mx(out=down_words[:, a, :].bitcast(FP8X4), scales=down_scale[:, a, :], in_=down_bf[:])
+
+        up_words = keep.tile([P, M], U32, name="up_words", align_bytes=64)
+        up_scale = keep.tile([P, M], U8, name="up_scale", align_bytes=64)
+
+        def quantize_up(u):
+            up_bf = keep.tile([P, PACK * BANK], BF16, name="up_bf%d" % u, align_bytes=64)
+            nc.scalar.copy(
+                out=up_bf[:].rearrange("p (c i j) -> p c j i", i=4, j=PACK),
+                in_=up_raw[u][:].rearrange("p j (c i) -> p c j i", i=4),
+            )
+            cols = slice(u * BANK, (u + 1) * BANK)
+            nc.vector.quantize_mx(out=up_words[:, cols].bitcast(FP8X4), scales=up_scale[:, cols], in_=up_bf[:])
+
+        quantize_up(0)
+
+        h_words = keep.tile([P, S], U32, name="h_words", align_bytes=64)
+        h_scale = keep.tile([P, S], U8, name="h_scale", align_bytes=64)
+        for half in range(HALVES):
+            h_bf = keep.tile([P, PACK * BANK], BF16, name="h_bf%d" % half, align_bytes=64)
+            for i in range(BANK // H_COLS):
+                cols = slice(half * BANK + i * H_COLS, half * BANK + (i + 1) * H_COLS)
+                h_bank = h_psum.tile([P, PACK, H_COLS], F32, name="h_bank")
+                for t in range(PACK):
+                    for a in range(PASSES):
+                        nc.tensor.matmul_mx(
+                            out=h_bank[:, t, :],
+                            lhsT=down_words[:, a, t * P : (t + 1) * P].bitcast(FP8X4),
+                            lhsT_scale=down_scale[:, a, t * P : (t + 1) * P],
+                            rhs=v_words[a][:, cols].bitcast(FP8X4),
+                            rhs_scale=v_scale[a][:, cols],
+                            start=(a == 0),
+                            stop=(a == PASSES - 1),
+                        )
+                nc.scalar.copy(
+                    out=h_bf[:, i * BANK : (i + 1) * BANK].rearrange("p (n t) -> p n t", t=PACK),
+                    in_=h_bank[:].rearrange("p t n -> p n t"),
+                )
+            cols = slice(half * BANK, (half + 1) * BANK)
+            nc.vector.quantize_mx(out=h_words[:, cols].bitcast(FP8X4), scales=h_scale[:, cols], in_=h_bf[:])
+
+        quantize_up(1)
+
+        result = [keep.tile([P, S], F32, name="result%d" % c) for c in range(ROW_TILES)]
+
+        def gather_residual(c):
+            step = BANK if c == ROW_TILES - 1 else S
+            for j0 in range(0, S, step):
+                nc.vector.tensor_copy(result[c][:, j0 : j0 + step], r_rows[c][:].indirect(list_part(j0, step)))
+
+        def finish(c):
+            rows = slice(c * P, (c + 1) * P)
+            for half in range(HALVES):
+                cols = slice(half * BANK, (half + 1) * BANK)
+                y_bank = y_psum.tile([P, BANK], F32, name="y_bank")
+                for a in range(PASSES):
+                    nc.tensor.matmul_mx(
+                        out=y_bank[:],
+                        lhsT=w4[:, a, 2 * c * P : 2 * (c + 1) * P].bitcast(FP4X4),
+                        lhsT_scale=w4_scale[:, a, :].bitcast(U8)[:, rows],
+                        rhs=v_words[a][:, cols].bitcast(FP8X4),
+                        rhs_scale=v_scale[a][:, cols],
+                        start=(a == 0),
+                        stop=False,
+                    )
+                nc.tensor.matmul_mx(
+                    out=y_bank[:],
+                    lhsT=up_words[:, rows].bitcast(FP8X4),
+                    lhsT_scale=up_scale[:, rows],
+                    rhs=h_words[:, cols].bitcast(FP8X4),
+                    rhs_scale=h_scale[:, cols],
+                    start=False,
+                    stop=True,
+                )
+                nc.vector.scalar_tensor_tensor(
+                    out=result[c][:, cols],
+                    in0=y_bank[:],
+                    scalar=bias[:, c : c + 1],
+                    in1=result[c][:, cols],
+                    op0=ADD,
+                    op1=ADD,
+                )
+                if c == ROW_TILES - 1:
+                    nc.sync.dma_start(out=out[rows, cols], in_=result[c][:, cols])
+            if c < ROW_TILES - 1:
+                nc.sync.dma_start(out=out[rows, :], in_=result[c][:])
+
+        gather_residual(0)
+        load_residual(ROW_TILES - 1)
+        for c in range(ROW_TILES):
+            if c + 1 < ROW_TILES:
+                gather_residual(c + 1)
+            finish(c)

@@ -15,6 +15,7 @@ U8 = mybir.dt.uint8
 FP8X4 = mybir.dt.float8_e4m3fn_x4
 FP4X4 = mybir.dt.float4_e2m1fn_x4
 ADD = mybir.AluOpType.add
+IDENTITY = mybir.ActivationFunctionType.Identity
 
 P = 128
 PACK = 4
@@ -25,6 +26,9 @@ HALVES = S // BANK
 ROW_TILES = M // P
 H_COLS = BANK // PACK
 LIST_ROWS = 16
+UP_COLS = 256
+GPSIMD_TILES = 6
+RESID_BUFS = 6
 
 
 def tile_list_tabres_bias_kernel(
@@ -33,7 +37,8 @@ def tile_list_tabres_bias_kernel(
     nc = tc.nc
     with ExitStack() as ctx:
         keep = ctx.enter_context(tc.tile_pool(name="keep", bufs=1))
-        resid = ctx.enter_context(tc.tile_pool(name="resid", bufs=7))
+        resid = ctx.enter_context(tc.tile_pool(name="resid", bufs=RESID_BUFS))
+        staged = ctx.enter_context(tc.tile_pool(name="staged", bufs=4))
         h_psum = ctx.enter_context(tc.psum_pool(name="h_psum", bufs=3))
         y_psum = ctx.enter_context(tc.psum_pool(name="y_psum", bufs=5))
 
@@ -51,21 +56,18 @@ def tile_list_tabres_bias_kernel(
         nc.vector.memset(b_rows[:], 0.0)
 
         def load_scales(queue, plane, source):
-            for q in range(4):
+            for r in range(4):
                 queue.dma_start(
-                    out=plane[32 * q : 32 * q + 4, :, :],
-                    in_=source[:, 4 * q : 4 * q + 4, :].bitcast(I32).rearrange("a r n -> r a n"),
+                    out=plane[r:P:32, :, :],
+                    in_=source[:, r:16:4, :].bitcast(I32).rearrange("a q n -> q a n"),
                 )
 
-        load_scales(nc.sync, tab_scale, tab_scales)
-        load_scales(nc.sync, w4_scale, w4_scales)
-        nc.sync.dma_start(out=b_rows[0:ROW_TILES, :], in_=b.rearrange("(c p) -> c p", p=P))
         identity = keep.tile([P, P], F32, name="identity")
         make_identity(nc, identity[:])
 
         table = [keep.tile([P, T], I32, name="table%d" % a, align_bytes=64) for a in range(PASSES)]
         down_raw = [keep.tile([P, PACK, R], F32, name="down_raw%d" % a) for a in range(PASSES)]
-        up_raw = [keep.tile([P, PACK, BANK], F32, name="up_raw%d" % u) for u in range(2)]
+        up_raw = keep.tile([P, PACK, M], F32, name="up_raw")
         w4 = keep.tile([P, PASSES, 2 * M], U8, name="w4", align_bytes=64)
         r_rows = {}
 
@@ -76,9 +78,8 @@ def tile_list_tabres_bias_kernel(
             rows = down[a * K_PASS : (a + 1) * K_PASS, :]
             nc.sync.dma_start(out=down_raw[a][:], in_=rows.rearrange("(p j) r -> p j r", j=PACK))
 
-        def load_up(u):
-            cols = up[:, u * BANK : (u + 1) * BANK]
-            nc.sync.dma_start(out=up_raw[u][:], in_=cols.rearrange("(p j) n -> p j n", j=PACK))
+        def load_up():
+            nc.sync.dma_start(out=up_raw[:], in_=up.rearrange("(p j) n -> p j n", j=PACK))
 
         def load_w4():
             nc.sync.dma_start(out=w4[:].bitcast(I32), in_=w4_words.bitcast(I32).rearrange("a p n -> p a n"))
@@ -88,24 +89,25 @@ def tile_list_tabres_bias_kernel(
             nc.sync.dma_start(out=r_rows[c][:], in_=rT[c * P : (c + 1) * P, :])
 
         load_table(0)
-        load_down(0)
+        load_scales(nc.sync, tab_scale, tab_scales)
         load_table(1)
+        load_down(0)
+        nc.sync.dma_start(out=b_rows[0:ROW_TILES, :], in_=b.rearrange("(c p) -> c p", p=P))
         load_down(1)
         load_down(2)
-        load_up(0)
         load_table(2)
+        load_up()
         load_residual(0)
         load_w4()
         load_residual(1)
-        load_residual(2)
-        load_up(1)
-        for c in range(3, 7):
+        load_scales(nc.sync, w4_scale, w4_scales)
+        for c in range(2, RESID_BUFS):
             load_residual(c)
 
         bias_t = h_psum.tile([P, P], F32, name="h_bank")
         nc.tensor.transpose(bias_t[:], b_rows[:], identity[:])
         bias = keep.tile([P, ROW_TILES], F32, name="bias")
-        nc.scalar.copy(out=bias[:], in_=bias_t[:, 0:ROW_TILES])
+        nc.scalar.activation(out=bias[:], in_=bias_t[:, 0:ROW_TILES], func=IDENTITY)
 
         v_words = [keep.tile([P, S], U32, name="v_words%d" % a, align_bytes=64) for a in range(PASSES)]
         v_scale = [keep.tile([P, S], U8, name="v_scale%d" % a, align_bytes=64) for a in range(PASSES)]
@@ -130,14 +132,13 @@ def tile_list_tabres_bias_kernel(
 
         def quantize_up(u):
             up_bf = keep.tile([P, PACK * BANK], BF16, name="up_bf%d" % u, align_bytes=64)
-            nc.scalar.copy(
-                out=up_bf[:].rearrange("p (c i j) -> p c j i", i=4, j=PACK),
-                in_=up_raw[u][:].rearrange("p j (c i) -> p c j i", i=4),
-            )
+            for n0 in range(0, BANK, UP_COLS):
+                nc.scalar.copy(
+                    out=up_bf[:, PACK * n0 : PACK * (n0 + UP_COLS)].rearrange("p (c i j) -> p c j i", i=4, j=PACK),
+                    in_=up_raw[:, :, u * BANK + n0 : u * BANK + n0 + UP_COLS].rearrange("p j (c i) -> p c j i", i=4),
+                )
             cols = slice(u * BANK, (u + 1) * BANK)
             nc.vector.quantize_mx(out=up_words[:, cols].bitcast(FP8X4), scales=up_scale[:, cols], in_=up_bf[:])
-
-        quantize_up(0)
 
         h_words = keep.tile([P, S], U32, name="h_words", align_bytes=64)
         h_scale = keep.tile([P, S], U8, name="h_scale", align_bytes=64)
@@ -164,6 +165,7 @@ def tile_list_tabres_bias_kernel(
             cols = slice(half * BANK, (half + 1) * BANK)
             nc.vector.quantize_mx(out=h_words[:, cols].bitcast(FP8X4), scales=h_scale[:, cols], in_=h_bf[:])
 
+        quantize_up(0)
         quantize_up(1)
 
         result = [keep.tile([P, S], F32, name="result%d" % c) for c in range(ROW_TILES)]
@@ -197,22 +199,28 @@ def tile_list_tabres_bias_kernel(
                     start=False,
                     stop=True,
                 )
-                nc.vector.scalar_tensor_tensor(
-                    out=result[c][:, cols],
-                    in0=y_bank[:],
-                    scalar=bias[:, c : c + 1],
-                    in1=result[c][:, cols],
-                    op0=ADD,
-                    op1=ADD,
-                )
+                if c < GPSIMD_TILES:
+                    y_biased = staged.tile([P, BANK], F32, name="y_biased")
+                    nc.scalar.activation(out=y_biased[:], in_=y_bank[:], func=IDENTITY, bias=bias[:, c : c + 1])
+                    nc.gpsimd.tensor_tensor(out=result[c][:, cols], in0=y_biased[:], in1=result[c][:, cols], op=ADD)
+                else:
+                    nc.vector.scalar_tensor_tensor(
+                        out=result[c][:, cols],
+                        in0=y_bank[:],
+                        scalar=bias[:, c : c + 1],
+                        in1=result[c][:, cols],
+                        op0=ADD,
+                        op1=ADD,
+                    )
                 if c == ROW_TILES - 1:
                     nc.sync.dma_start(out=out[rows, cols], in_=result[c][:, cols])
             if c < ROW_TILES - 1:
                 nc.sync.dma_start(out=out[rows, :], in_=result[c][:])
 
-        gather_residual(0)
-        load_residual(ROW_TILES - 1)
+        for c in range(ROW_TILES - RESID_BUFS):
+            gather_residual(c)
+            load_residual(RESID_BUFS + c)
         for c in range(ROW_TILES):
-            if c + 1 < ROW_TILES:
+            if ROW_TILES - RESID_BUFS <= c + 1 < ROW_TILES:
                 gather_residual(c + 1)
             finish(c)

@@ -27,7 +27,7 @@ ROW_TILES = M // P
 H_COLS = BANK // PACK
 LIST_ROWS = 16
 UP_COLS = 256
-GPSIMD_TILES = 6
+GPSIMD_BANKS = 13
 RESID_BUFS = 6
 
 
@@ -99,9 +99,8 @@ def tile_list_tabres_bias_kernel(
         load_up()
         load_residual(0)
         load_w4()
-        load_residual(1)
         load_scales(nc.sync, w4_scale, w4_scales)
-        for c in range(2, RESID_BUFS):
+        for c in range(1, RESID_BUFS):
             load_residual(c)
 
         bias_t = h_psum.tile([P, P], F32, name="h_bank")
@@ -113,12 +112,14 @@ def tile_list_tabres_bias_kernel(
         v_scale = [keep.tile([P, S], U8, name="v_scale%d" % a, align_bytes=64) for a in range(PASSES)]
         down_words = keep.tile([P, PASSES, R], U32, name="down_words", align_bytes=64)
         down_scale = keep.tile([P, PASSES, R], U8, name="down_scale", align_bytes=64)
+
+        def gather_words(a, j0, count):
+            nc.vector.tensor_copy(
+                v_words[a][:, j0 : j0 + count], table[a][:].bitcast(U32).indirect(list_part(j0, count))
+            )
+
         for a in range(PASSES):
-            step = BANK if a == PASSES - 1 else S
-            for j0 in range(0, S, step):
-                nc.vector.tensor_copy(
-                    v_words[a][:, j0 : j0 + step], table[a][:].bitcast(U32).indirect(list_part(j0, step))
-                )
+            gather_words(a, 0, BANK if a == PASSES - 1 else S)
             nc.vector.tensor_copy(v_scale[a][:], tab_scale[:, a, :].bitcast(U8).indirect(offsets[:]))
             down_bf = keep.tile([P, PACK * R], BF16, name="down_bf%d" % a, align_bytes=64)
             nc.scalar.copy(
@@ -126,22 +127,32 @@ def tile_list_tabres_bias_kernel(
                 in_=down_raw[a][:].rearrange("p j (m t) -> p m j t", t=PACK),
             )
             nc.vector.quantize_mx(out=down_words[:, a, :].bitcast(FP8X4), scales=down_scale[:, a, :], in_=down_bf[:])
+        gather_words(PASSES - 1, BANK, BANK)
 
         up_words = keep.tile([P, M], U32, name="up_words", align_bytes=64)
         up_scale = keep.tile([P, M], U8, name="up_scale", align_bytes=64)
 
         def quantize_up(u):
             up_bf = keep.tile([P, PACK * BANK], BF16, name="up_bf%d" % u, align_bytes=64)
+            cast = nc.scalar.copy if u == 0 else nc.vector.tensor_copy
             for n0 in range(0, BANK, UP_COLS):
-                nc.scalar.copy(
+                cast(
                     out=up_bf[:, PACK * n0 : PACK * (n0 + UP_COLS)].rearrange("p (c i j) -> p c j i", i=4, j=PACK),
                     in_=up_raw[:, :, u * BANK + n0 : u * BANK + n0 + UP_COLS].rearrange("p j (c i) -> p c j i", i=4),
                 )
             cols = slice(u * BANK, (u + 1) * BANK)
             nc.vector.quantize_mx(out=up_words[:, cols].bitcast(FP8X4), scales=up_scale[:, cols], in_=up_bf[:])
 
+        result = [keep.tile([P, S], F32, name="result%d" % c) for c in range(ROW_TILES)]
+
+        def gather_residual(c):
+            step = BANK if c == ROW_TILES - 1 else S
+            for j0 in range(0, S, step):
+                nc.vector.tensor_copy(result[c][:, j0 : j0 + step], r_rows[c][:].indirect(list_part(j0, step)))
+
         h_words = keep.tile([P, S], U32, name="h_words", align_bytes=64)
         h_scale = keep.tile([P, S], U8, name="h_scale", align_bytes=64)
+        h_bfs = []
         for half in range(HALVES):
             h_bf = keep.tile([P, PACK * BANK], BF16, name="h_bf%d" % half, align_bytes=64)
             for i in range(BANK // H_COLS):
@@ -162,18 +173,14 @@ def tile_list_tabres_bias_kernel(
                     out=h_bf[:, i * BANK : (i + 1) * BANK].rearrange("p (n t) -> p n t", t=PACK),
                     in_=h_bank[:].rearrange("p t n -> p n t"),
                 )
+            h_bfs.append(h_bf)
+
+        def quantize_h(half):
             cols = slice(half * BANK, (half + 1) * BANK)
-            nc.vector.quantize_mx(out=h_words[:, cols].bitcast(FP8X4), scales=h_scale[:, cols], in_=h_bf[:])
+            nc.vector.quantize_mx(out=h_words[:, cols].bitcast(FP8X4), scales=h_scale[:, cols], in_=h_bfs[half][:])
 
         quantize_up(0)
         quantize_up(1)
-
-        result = [keep.tile([P, S], F32, name="result%d" % c) for c in range(ROW_TILES)]
-
-        def gather_residual(c):
-            step = BANK if c == ROW_TILES - 1 else S
-            for j0 in range(0, S, step):
-                nc.vector.tensor_copy(result[c][:, j0 : j0 + step], r_rows[c][:].indirect(list_part(j0, step)))
 
         def finish(c):
             rows = slice(c * P, (c + 1) * P)
@@ -199,7 +206,7 @@ def tile_list_tabres_bias_kernel(
                     start=False,
                     stop=True,
                 )
-                if c < GPSIMD_TILES:
+                if c * HALVES + half < GPSIMD_BANKS:
                     y_biased = staged.tile([P, BANK], F32, name="y_biased")
                     nc.scalar.activation(out=y_biased[:], in_=y_bank[:], func=IDENTITY, bias=bias[:, c : c + 1])
                     nc.gpsimd.tensor_tensor(out=result[c][:, cols], in0=y_biased[:], in1=result[c][:, cols], op=ADD)
@@ -217,10 +224,13 @@ def tile_list_tabres_bias_kernel(
             if c < ROW_TILES - 1:
                 nc.sync.dma_start(out=out[rows, :], in_=result[c][:])
 
-        for c in range(ROW_TILES - RESID_BUFS):
-            gather_residual(c)
-            load_residual(RESID_BUFS + c)
+        gather_residual(0)
+        load_residual(6)
+        quantize_h(0)
+        quantize_h(1)
+        gather_residual(1)
+        load_residual(7)
         for c in range(ROW_TILES):
-            if ROW_TILES - RESID_BUFS <= c + 1 < ROW_TILES:
+            if 2 <= c + 1 < ROW_TILES:
                 gather_residual(c + 1)
             finish(c)

@@ -28,7 +28,11 @@ H_COLS = BANK // PACK
 LIST_ROWS = 16
 UP_COLS = 256
 GPSIMD_BANKS = 13
-RESID_BUFS = 6
+SCALE_ROWS = 16
+ROW_STEP = 6
+PASS_STEP = 8
+LOAD_BUFS = 13
+LAST_GATHER = 256
 
 
 def tile_list_tabres_bias_kernel(
@@ -37,10 +41,9 @@ def tile_list_tabres_bias_kernel(
     nc = tc.nc
     with ExitStack() as ctx:
         keep = ctx.enter_context(tc.tile_pool(name="keep", bufs=1))
-        resid = ctx.enter_context(tc.tile_pool(name="resid", bufs=RESID_BUFS))
+        loads = ctx.enter_context(tc.tile_pool(name="loads", bufs=LOAD_BUFS))
         staged = ctx.enter_context(tc.tile_pool(name="staged", bufs=4))
-        h_psum = ctx.enter_context(tc.psum_pool(name="h_psum", bufs=3))
-        y_psum = ctx.enter_context(tc.psum_pool(name="y_psum", bufs=5))
+        psum = ctx.enter_context(tc.psum_pool(name="psum", bufs=8))
 
         offsets = keep.tile([P, S // LIST_ROWS], U16, name="offsets")
         nc.sync.dma_start(offsets[:], offs)
@@ -48,33 +51,53 @@ def tile_list_tabres_bias_kernel(
         def list_part(first, count):
             return offsets[:, first // LIST_ROWS : (first + count) // LIST_ROWS]
 
-        w4_scale = keep.tile([P, PASSES, M // 4], I32, name="w4_scale", align_bytes=64)
-        tab_scale = keep.tile([P, PASSES, T // 4], I32, name="tab_scale", align_bytes=64)
-        nc.vector.memset(tab_scale[:], 0)
-        nc.gpsimd.memset(w4_scale[:], 0)
         b_rows = keep.tile([P, P], F32, name="b_rows")
-        nc.vector.memset(b_rows[:], 0.0)
+        nc.gpsimd.memset(b_rows[:], 0.0)
+        tab_scale = keep.tile([P, T // 4], I32, name="tab_scale", align_bytes=64)
+        nc.gpsimd.memset(tab_scale[:], 0)
+        v_scale = keep.tile([P, PASSES, S // 4], I32, name="v_scale", align_bytes=64)
+        w4_scale = keep.tile([P, PASSES, M // 4], I32, name="w4_scale", align_bytes=64)
+        nc.vector.memset(v_scale[:], 0)
+        nc.vector.memset(w4_scale[:], 0)
+        picked_scale = keep.tile([P, S], U8, name="picked_scale", align_bytes=64)
 
-        def load_scales(queue, plane, source):
+        def load_table_scales():
+            for a in range(PASSES):
+                first = PASS_STEP * a
+                nc.sync.dma_start(
+                    out=tab_scale[first : first + ROW_STEP * SCALE_ROWS : ROW_STEP, :], in_=tab_scales[a].bitcast(I32)
+                )
+
+        def place_table_scales(rows):
+            for r in rows:
+                first = ROW_STEP * r
+                nc.sync.dma_start(
+                    out=v_scale[r:P:32, :, :],
+                    in_=picked_scale[first : first + PASS_STEP * 4 * PASSES : PASS_STEP, :].bitcast(I32),
+                )
+
+        def load_w4_scales():
             for r in range(4):
-                queue.dma_start(
-                    out=plane[r:P:32, :, :],
-                    in_=source[:, r:16:4, :].bitcast(I32).rearrange("a q n -> q a n"),
+                nc.sync.dma_start(
+                    out=w4_scale[r:P:32, :, :],
+                    in_=w4_scales[:, r:16:4, :].bitcast(I32).rearrange("a q n -> q a n"),
                 )
 
         identity = keep.tile([P, P], F32, name="identity")
         make_identity(nc, identity[:])
 
-        table = [keep.tile([P, T], I32, name="table%d" % a, align_bytes=64) for a in range(PASSES)]
-        down_raw = [keep.tile([P, PACK, R], F32, name="down_raw%d" % a) for a in range(PASSES)]
+        table = {}
+        down_raw = {}
         up_raw = keep.tile([P, PACK, M], F32, name="up_raw")
         w4 = keep.tile([P, PASSES, 2 * M], U8, name="w4", align_bytes=64)
         r_rows = {}
 
         def load_table(a):
+            table[a] = loads.tile([P, T], I32, name="loaded")
             nc.sync.dma_start(out=table[a][:], in_=tab_words[a].rearrange("p t i -> p (t i)").bitcast(I32))
 
         def load_down(a):
+            down_raw[a] = loads.tile([P, PACK, R], F32, name="loaded")
             rows = down[a * K_PASS : (a + 1) * K_PASS, :]
             nc.sync.dma_start(out=down_raw[a][:], in_=rows.rearrange("(p j) r -> p j r", j=PACK))
 
@@ -85,31 +108,33 @@ def tile_list_tabres_bias_kernel(
             nc.sync.dma_start(out=w4[:].bitcast(I32), in_=w4_words.bitcast(I32).rearrange("a p n -> p a n"))
 
         def load_residual(c):
-            r_rows[c] = resid.tile([P, T], F32, name="r_rows")
+            r_rows[c] = loads.tile([P, T], F32, name="loaded")
             nc.sync.dma_start(out=r_rows[c][:], in_=rT[c * P : (c + 1) * P, :])
 
-        load_table(0)
-        load_scales(nc.sync, tab_scale, tab_scales)
-        load_table(1)
-        load_down(0)
         nc.sync.dma_start(out=b_rows[0:ROW_TILES, :], in_=b.rearrange("(c p) -> c p", p=P))
+        load_table_scales()
+        load_table(0)
+        load_down(0)
         load_down(1)
+        nc.vector.tensor_copy(picked_scale[:], tab_scale[:].bitcast(U8).indirect(offsets[:]))
+        place_table_scales((0, 1))
+        load_table(1)
+        place_table_scales((2, 3))
         load_down(2)
         load_table(2)
         load_up()
         load_residual(0)
         load_w4()
-        load_scales(nc.sync, w4_scale, w4_scales)
-        for c in range(1, RESID_BUFS):
+        load_w4_scales()
+        for c in range(1, ROW_TILES):
             load_residual(c)
 
-        bias_t = h_psum.tile([P, P], F32, name="h_bank")
+        bias_t = psum.tile([P, P], F32, name="bank")
         nc.tensor.transpose(bias_t[:], b_rows[:], identity[:])
         bias = keep.tile([P, ROW_TILES], F32, name="bias")
         nc.scalar.activation(out=bias[:], in_=bias_t[:, 0:ROW_TILES], func=IDENTITY)
 
         v_words = [keep.tile([P, S], U32, name="v_words%d" % a, align_bytes=64) for a in range(PASSES)]
-        v_scale = [keep.tile([P, S], U8, name="v_scale%d" % a, align_bytes=64) for a in range(PASSES)]
         down_words = keep.tile([P, PASSES, R], U32, name="down_words", align_bytes=64)
         down_scale = keep.tile([P, PASSES, R], U8, name="down_scale", align_bytes=64)
 
@@ -118,25 +143,29 @@ def tile_list_tabres_bias_kernel(
                 v_words[a][:, j0 : j0 + count], table[a][:].bitcast(U32).indirect(list_part(j0, count))
             )
 
-        for a in range(PASSES):
-            gather_words(a, 0, BANK if a == PASSES - 1 else S)
-            nc.vector.tensor_copy(v_scale[a][:], tab_scale[:, a, :].bitcast(U8).indirect(offsets[:]))
+        def quantize_down(a):
             down_bf = keep.tile([P, PACK * R], BF16, name="down_bf%d" % a, align_bytes=64)
             nc.scalar.copy(
                 out=down_bf[:].rearrange("p (t m j) -> p m j t", t=PACK, j=PACK),
                 in_=down_raw[a][:].rearrange("p j (m t) -> p m j t", t=PACK),
             )
             nc.vector.quantize_mx(out=down_words[:, a, :].bitcast(FP8X4), scales=down_scale[:, a, :], in_=down_bf[:])
-        gather_words(PASSES - 1, BANK, BANK)
+
+        gather_words(0, 0, S)
+        quantize_down(0)
+        quantize_down(1)
+        gather_words(1, 0, S)
+        quantize_down(2)
+        for j0 in range(0, S, LAST_GATHER):
+            gather_words(PASSES - 1, j0, LAST_GATHER)
 
         up_words = keep.tile([P, M], U32, name="up_words", align_bytes=64)
         up_scale = keep.tile([P, M], U8, name="up_scale", align_bytes=64)
 
         def quantize_up(u):
             up_bf = keep.tile([P, PACK * BANK], BF16, name="up_bf%d" % u, align_bytes=64)
-            cast = nc.scalar.copy if u == 0 else nc.vector.tensor_copy
             for n0 in range(0, BANK, UP_COLS):
-                cast(
+                nc.scalar.copy(
                     out=up_bf[:, PACK * n0 : PACK * (n0 + UP_COLS)].rearrange("p (c i j) -> p c j i", i=4, j=PACK),
                     in_=up_raw[:, :, u * BANK + n0 : u * BANK + n0 + UP_COLS].rearrange("p j (c i) -> p c j i", i=4),
                 )
@@ -152,48 +181,45 @@ def tile_list_tabres_bias_kernel(
 
         h_words = keep.tile([P, S], U32, name="h_words", align_bytes=64)
         h_scale = keep.tile([P, S], U8, name="h_scale", align_bytes=64)
-        h_bfs = []
-        for half in range(HALVES):
-            h_bf = keep.tile([P, PACK * BANK], BF16, name="h_bf%d" % half, align_bytes=64)
-            for i in range(BANK // H_COLS):
-                cols = slice(half * BANK + i * H_COLS, half * BANK + (i + 1) * H_COLS)
-                h_bank = h_psum.tile([P, PACK, H_COLS], F32, name="h_bank")
+        h_bfs = [keep.tile([P, PACK * BANK], BF16, name="h_bf%d" % half, align_bytes=64) for half in range(HALVES)]
+        h_banks = [psum.tile([P, PACK, H_COLS], F32, name="bank") for i in range(S // H_COLS)]
+        for a in range(PASSES):
+            for i, h_bank in enumerate(h_banks):
+                cols = slice(i * H_COLS, (i + 1) * H_COLS)
                 for t in range(PACK):
-                    for a in range(PASSES):
-                        nc.tensor.matmul_mx(
-                            out=h_bank[:, t, :],
-                            lhsT=down_words[:, a, t * P : (t + 1) * P].bitcast(FP8X4),
-                            lhsT_scale=down_scale[:, a, t * P : (t + 1) * P],
-                            rhs=v_words[a][:, cols].bitcast(FP8X4),
-                            rhs_scale=v_scale[a][:, cols],
-                            start=(a == 0),
-                            stop=(a == PASSES - 1),
-                        )
-                nc.scalar.copy(
-                    out=h_bf[:, i * BANK : (i + 1) * BANK].rearrange("p (n t) -> p n t", t=PACK),
-                    in_=h_bank[:].rearrange("p t n -> p n t"),
-                )
-            h_bfs.append(h_bf)
+                    nc.tensor.matmul_mx(
+                        out=h_bank[:, t, :],
+                        lhsT=down_words[:, a, t * P : (t + 1) * P].bitcast(FP8X4),
+                        lhsT_scale=down_scale[:, a, t * P : (t + 1) * P],
+                        rhs=v_words[a][:, cols].bitcast(FP8X4),
+                        rhs_scale=v_scale[:, a, :].bitcast(U8)[:, cols],
+                        start=(a == 0 and t == 0),
+                        stop=(a == PASSES - 1 and t == PACK - 1),
+                    )
+        for i, h_bank in enumerate(h_banks):
+            half, part = divmod(i, PACK)
+            copy = nc.scalar.copy if half == 0 else nc.vector.tensor_copy
+            copy(
+                out=h_bfs[half][:, part * BANK : (part + 1) * BANK].rearrange("p (n t) -> p n t", t=PACK),
+                in_=h_bank[:].rearrange("p t n -> p n t"),
+            )
 
         def quantize_h(half):
             cols = slice(half * BANK, (half + 1) * BANK)
             nc.vector.quantize_mx(out=h_words[:, cols].bitcast(FP8X4), scales=h_scale[:, cols], in_=h_bfs[half][:])
 
-        quantize_up(0)
-        quantize_up(1)
-
         def finish(c):
             rows = slice(c * P, (c + 1) * P)
             for half in range(HALVES):
                 cols = slice(half * BANK, (half + 1) * BANK)
-                y_bank = y_psum.tile([P, BANK], F32, name="y_bank")
+                y_bank = psum.tile([P, BANK], F32, name="bank")
                 for a in range(PASSES):
                     nc.tensor.matmul_mx(
                         out=y_bank[:],
                         lhsT=w4[:, a, 2 * c * P : 2 * (c + 1) * P].bitcast(FP4X4),
                         lhsT_scale=w4_scale[:, a, :].bitcast(U8)[:, rows],
                         rhs=v_words[a][:, cols].bitcast(FP8X4),
-                        rhs_scale=v_scale[a][:, cols],
+                        rhs_scale=v_scale[:, a, :].bitcast(U8)[:, cols],
                         start=(a == 0),
                         stop=False,
                     )
@@ -224,13 +250,12 @@ def tile_list_tabres_bias_kernel(
             if c < ROW_TILES - 1:
                 nc.sync.dma_start(out=out[rows, :], in_=result[c][:])
 
-        gather_residual(0)
-        load_residual(6)
         quantize_h(0)
         quantize_h(1)
-        gather_residual(1)
-        load_residual(7)
+        quantize_up(0)
+        gather_residual(0)
+        quantize_up(1)
         for c in range(ROW_TILES):
-            if 2 <= c + 1 < ROW_TILES:
+            if c + 1 < ROW_TILES:
                 gather_residual(c + 1)
             finish(c)

@@ -31,7 +31,8 @@ GPSIMD_BANKS = 13
 SCALE_ROWS = 16
 ROW_STEP = 6
 PASS_STEP = 8
-LOAD_BUFS = 13
+LOAD_BUFS = 12
+HEAD_COLS = T // 4
 LAST_GATHER = 256
 
 
@@ -51,10 +52,10 @@ def tile_list_tabres_bias_kernel(
         def list_part(first, count):
             return offsets[:, first // LIST_ROWS : (first + count) // LIST_ROWS]
 
-        b_rows = keep.tile([P, P], F32, name="b_rows")
-        nc.gpsimd.memset(b_rows[:], 0.0)
         tab_scale = keep.tile([P, T // 4], I32, name="tab_scale", align_bytes=64)
         nc.gpsimd.memset(tab_scale[:], 0)
+        b_rows = keep.tile([P, P], F32, name="b_rows")
+        nc.vector.memset(b_rows[:], 0.0)
         v_scale = keep.tile([P, PASSES, S // 4], I32, name="v_scale", align_bytes=64)
         w4_scale = keep.tile([P, PASSES, M // 4], I32, name="w4_scale", align_bytes=64)
         nc.vector.memset(v_scale[:], 0)
@@ -92,9 +93,11 @@ def tile_list_tabres_bias_kernel(
         w4 = keep.tile([P, PASSES, 2 * M], U8, name="w4", align_bytes=64)
         r_rows = {}
 
-        def load_table(a):
-            table[a] = loads.tile([P, T], I32, name="loaded")
-            nc.sync.dma_start(out=table[a][:], in_=tab_words[a].rearrange("p t i -> p (t i)").bitcast(I32))
+        def load_table(a, first=0, last=T):
+            if first == 0:
+                table[a] = loads.tile([P, T], I32, name="loaded")
+            words = tab_words[a].rearrange("p t i -> p (t i)").bitcast(I32)
+            nc.sync.dma_start(out=table[a][:, first:last], in_=words[:, first:last])
 
         def load_down(a):
             down_raw[a] = loads.tile([P, PACK, R], F32, name="loaded")
@@ -108,12 +111,16 @@ def tile_list_tabres_bias_kernel(
             nc.sync.dma_start(out=w4[:].bitcast(I32), in_=w4_words.bitcast(I32).rearrange("a p n -> p a n"))
 
         def load_residual(c):
-            r_rows[c] = loads.tile([P, T], F32, name="loaded")
+            if c == 0:
+                r_rows[c] = keep.tile([P, T], F32, name="first_rows", align_bytes=64)
+            else:
+                r_rows[c] = loads.tile([P, T], F32, name="loaded")
             nc.sync.dma_start(out=r_rows[c][:], in_=rT[c * P : (c + 1) * P, :])
 
-        nc.sync.dma_start(out=b_rows[0:ROW_TILES, :], in_=b.rearrange("(c p) -> c p", p=P))
+        load_table(0, 0, HEAD_COLS)
         load_table_scales()
-        load_table(0)
+        load_table(0, HEAD_COLS, T)
+        nc.sync.dma_start(out=b_rows[0:ROW_TILES, :], in_=b.rearrange("(c p) -> c p", p=P))
         load_down(0)
         load_down(1)
         nc.vector.tensor_copy(picked_scale[:], tab_scale[:].bitcast(U8).indirect(offsets[:]))
@@ -122,10 +129,10 @@ def tile_list_tabres_bias_kernel(
         place_table_scales((2, 3))
         load_down(2)
         load_table(2)
-        load_up()
-        load_residual(0)
         load_w4()
         load_w4_scales()
+        load_residual(0)
+        load_up()
         for c in range(1, ROW_TILES):
             load_residual(c)
 
@@ -159,27 +166,29 @@ def tile_list_tabres_bias_kernel(
         for j0 in range(0, S, LAST_GATHER):
             gather_words(PASSES - 1, j0, LAST_GATHER)
 
+        result = [keep.tile([P, S], F32, name="result%d" % c) for c in range(ROW_TILES)]
         up_words = keep.tile([P, M], U32, name="up_words", align_bytes=64)
         up_scale = keep.tile([P, M], U8, name="up_scale", align_bytes=64)
 
         def quantize_up(u):
             up_bf = keep.tile([P, PACK * BANK], BF16, name="up_bf%d" % u, align_bytes=64)
+            cast = nc.vector.tensor_copy if u == 0 else nc.scalar.copy
             for n0 in range(0, BANK, UP_COLS):
-                nc.scalar.copy(
+                cast(
                     out=up_bf[:, PACK * n0 : PACK * (n0 + UP_COLS)].rearrange("p (c i j) -> p c j i", i=4, j=PACK),
                     in_=up_raw[:, :, u * BANK + n0 : u * BANK + n0 + UP_COLS].rearrange("p j (c i) -> p c j i", i=4),
                 )
             cols = slice(u * BANK, (u + 1) * BANK)
             nc.vector.quantize_mx(out=up_words[:, cols].bitcast(FP8X4), scales=up_scale[:, cols], in_=up_bf[:])
 
-        result = [keep.tile([P, S], F32, name="result%d" % c) for c in range(ROW_TILES)]
 
         def gather_residual(c):
             step = BANK if c == ROW_TILES - 1 else S
             for j0 in range(0, S, step):
                 nc.vector.tensor_copy(result[c][:, j0 : j0 + step], r_rows[c][:].indirect(list_part(j0, step)))
 
-        h_words = keep.tile([P, S], U32, name="h_words", align_bytes=64)
+        gather_residual(0)
+        h_words = keep.tile([P, S], U32, name="first_rows", align_bytes=64)
         h_scale = keep.tile([P, S], U8, name="h_scale", align_bytes=64)
         h_bfs = [keep.tile([P, PACK * BANK], BF16, name="h_bf%d" % half, align_bytes=64) for half in range(HALVES)]
         h_banks = [psum.tile([P, PACK, H_COLS], F32, name="bank") for i in range(S // H_COLS)]
@@ -198,8 +207,7 @@ def tile_list_tabres_bias_kernel(
                     )
         for i, h_bank in enumerate(h_banks):
             half, part = divmod(i, PACK)
-            copy = nc.scalar.copy if half == 0 else nc.vector.tensor_copy
-            copy(
+            nc.scalar.copy(
                 out=h_bfs[half][:, part * BANK : (part + 1) * BANK].rearrange("p (n t) -> p n t", t=PACK),
                 in_=h_bank[:].rearrange("p t n -> p n t"),
             )
@@ -253,7 +261,6 @@ def tile_list_tabres_bias_kernel(
         quantize_h(0)
         quantize_h(1)
         quantize_up(0)
-        gather_residual(0)
         quantize_up(1)
         for c in range(ROW_TILES):
             if c + 1 < ROW_TILES:

@@ -31,7 +31,8 @@ GPSIMD_BANKS = 13
 SCALE_ROWS = 16
 ROW_STEP = 6
 PASS_STEP = 8
-LOAD_BUFS = 12
+RESIDUAL_LOADS = ((0,), (1,), (2,), (3,), (4,), (5,), (6,), (7,))
+STORES = ((0, 1, 2), (3, 4), (5,), (6,), (7,))
 HEAD_COLS = T // 4
 LAST_GATHER = 256
 
@@ -42,7 +43,6 @@ def tile_list_tabres_bias_kernel(
     nc = tc.nc
     with ExitStack() as ctx:
         keep = ctx.enter_context(tc.tile_pool(name="keep", bufs=1))
-        loads = ctx.enter_context(tc.tile_pool(name="loads", bufs=LOAD_BUFS))
         staged = ctx.enter_context(tc.tile_pool(name="staged", bufs=4))
         psum = ctx.enter_context(tc.psum_pool(name="psum", bufs=8))
 
@@ -87,54 +87,61 @@ def tile_list_tabres_bias_kernel(
         identity = keep.tile([P, P], F32, name="identity")
         make_identity(nc, identity[:])
 
-        table = {}
+        table = [keep.tile([P, T], I32, name="table%d" % a) for a in range(PASSES)]
         down_raw = {}
         up_raw = keep.tile([P, PACK, M], F32, name="up_raw")
         w4 = keep.tile([P, PASSES, 2 * M], U8, name="w4", align_bytes=64)
         r_rows = {}
 
         def load_table(a, first=0, last=T):
-            if first == 0:
-                table[a] = loads.tile([P, T], I32, name="loaded")
             words = tab_words[a].rearrange("p t i -> p (t i)").bitcast(I32)
             nc.sync.dma_start(out=table[a][:, first:last], in_=words[:, first:last])
 
-        def load_down(a):
-            down_raw[a] = loads.tile([P, PACK, R], F32, name="loaded")
-            rows = down[a * K_PASS : (a + 1) * K_PASS, :]
-            nc.sync.dma_start(out=down_raw[a][:], in_=rows.rearrange("(p j) r -> p j r", j=PACK))
+        def load_down(first, count):
+            raw = keep.tile([P, count, PACK * R], F32, name="down_raw%d" % first)
+            rows = down[first * K_PASS : (first + count) * K_PASS, :]
+            nc.sync.dma_start(out=raw[:], in_=rows.rearrange("(a p j) r -> p a (j r)", p=P, j=PACK))
+            for a in range(count):
+                down_raw[first + a] = raw[:, a, :]
 
         def load_up():
             nc.sync.dma_start(out=up_raw[:], in_=up.rearrange("(p j) n -> p j n", j=PACK))
 
-        def load_w4():
-            nc.sync.dma_start(out=w4[:].bitcast(I32), in_=w4_words.bitcast(I32).rearrange("a p n -> p a n"))
+        def load_w4(first, last):
+            words = w4_words[first:last].bitcast(I32).rearrange("a p n -> p a n")
+            nc.sync.dma_start(out=w4[:, first:last, :].bitcast(I32), in_=words)
 
-        def load_residual(c):
-            if c == 0:
-                r_rows[c] = keep.tile([P, T], F32, name="first_rows", align_bytes=64)
+        buffer_of = {0: "first_rows", 1: "table0", 2: "down_raw0", 7: "table1"}
+
+        def load_residual(tiles):
+            first, count = tiles[0], len(tiles)
+            name = buffer_of.get(first, "r_rows%d" % first)
+            if first == 0:
+                raw = keep.tile([P, count, T], F32, name=name, align_bytes=64)
             else:
-                r_rows[c] = loads.tile([P, T], F32, name="loaded")
-            nc.sync.dma_start(out=r_rows[c][:], in_=rT[c * P : (c + 1) * P, :])
+                raw = keep.tile([P, count, T], F32, name=name)
+            rows = rT[first * P : (first + count) * P, :]
+            nc.sync.dma_start(out=raw[:], in_=rows.rearrange("(c p) t -> p c t", p=P))
+            for c in range(count):
+                r_rows[first + c] = raw[:, c, :]
 
         load_table(0, 0, HEAD_COLS)
         load_table_scales()
         load_table(0, HEAD_COLS, T)
         nc.sync.dma_start(out=b_rows[0:ROW_TILES, :], in_=b.rearrange("(c p) -> c p", p=P))
-        load_down(0)
-        load_down(1)
+        load_down(0, 1)
+        load_down(1, 1)
         nc.vector.tensor_copy(picked_scale[:], tab_scale[:].bitcast(U8).indirect(offsets[:]))
         place_table_scales((0, 1))
         load_table(1)
         place_table_scales((2, 3))
-        load_down(2)
+        load_down(2, 1)
         load_table(2)
-        load_w4()
+        load_residual(RESIDUAL_LOADS[0])
         load_w4_scales()
-        load_residual(0)
+        load_w4(0, 1)
         load_up()
-        for c in range(1, ROW_TILES):
-            load_residual(c)
+        load_w4(1, PASSES)
 
         bias_t = psum.tile([P, P], F32, name="bank")
         nc.tensor.transpose(bias_t[:], b_rows[:], identity[:])
@@ -154,7 +161,7 @@ def tile_list_tabres_bias_kernel(
             down_bf = keep.tile([P, PACK * R], BF16, name="down_bf%d" % a, align_bytes=64)
             nc.scalar.copy(
                 out=down_bf[:].rearrange("p (t m j) -> p m j t", t=PACK, j=PACK),
-                in_=down_raw[a][:].rearrange("p j (m t) -> p m j t", t=PACK),
+                in_=down_raw[a].rearrange("p (j m t) -> p m j t", j=PACK, t=PACK),
             )
             nc.vector.quantize_mx(out=down_words[:, a, :].bitcast(FP8X4), scales=down_scale[:, a, :], in_=down_bf[:])
 
@@ -166,7 +173,12 @@ def tile_list_tabres_bias_kernel(
         for j0 in range(0, S, LAST_GATHER):
             gather_words(PASSES - 1, j0, LAST_GATHER)
 
-        result = [keep.tile([P, S], F32, name="result%d" % c) for c in range(ROW_TILES)]
+        for tiles in RESIDUAL_LOADS[1:]:
+            load_residual(tiles)
+
+        store_size = {tiles[-1]: len(tiles) for tiles in STORES}
+        stored = {tiles[-1]: keep.tile([P, len(tiles), S], F32, name="result%d" % tiles[0]) for tiles in STORES}
+        result = {c: stored[tiles[-1]][:, c - tiles[0], :] for tiles in STORES for c in tiles}
         up_words = keep.tile([P, M], U32, name="up_words", align_bytes=64)
         up_scale = keep.tile([P, M], U8, name="up_scale", align_bytes=64)
 
@@ -183,9 +195,7 @@ def tile_list_tabres_bias_kernel(
 
 
         def gather_residual(c):
-            step = BANK if c == ROW_TILES - 1 else S
-            for j0 in range(0, S, step):
-                nc.vector.tensor_copy(result[c][:, j0 : j0 + step], r_rows[c][:].indirect(list_part(j0, step)))
+            nc.vector.tensor_copy(result[c], r_rows[c].indirect(offsets[:]))
 
         gather_residual(0)
         h_words = keep.tile([P, S], U32, name="first_rows", align_bytes=64)
@@ -253,10 +263,10 @@ def tile_list_tabres_bias_kernel(
                         op0=ADD,
                         op1=ADD,
                     )
-                if c == ROW_TILES - 1:
-                    nc.sync.dma_start(out=out[rows, cols], in_=result[c][:, cols])
-            if c < ROW_TILES - 1:
-                nc.sync.dma_start(out=out[rows, :], in_=result[c][:])
+            if c in stored:
+                count = store_size[c]
+                written = out[(c + 1 - count) * P : (c + 1) * P, :]
+                nc.sync.dma_start(out=written.rearrange("(c p) j -> p c j", p=P), in_=stored[c][:])
 
         quantize_h(0)
         quantize_h(1)

@@ -53,7 +53,7 @@ def tile_list_tabres_bias_kernel(
             return offsets[:, first // LIST_ROWS : (first + count) // LIST_ROWS]
 
         tab_scale = keep.tile([P, T // 4], I32, name="tab_scale", align_bytes=64)
-        nc.gpsimd.memset(tab_scale[:], 0)
+        nc.vector.memset(tab_scale[:], 0)
         b_rows = keep.tile([P, P], F32, name="b_rows")
         nc.vector.memset(b_rows[:], 0.0)
         v_scale = keep.tile([P, PASSES, S // 4], I32, name="v_scale", align_bytes=64)
@@ -69,8 +69,8 @@ def tile_list_tabres_bias_kernel(
                     out=tab_scale[first : first + ROW_STEP * SCALE_ROWS : ROW_STEP, :], in_=tab_scales[a].bitcast(I32)
                 )
 
-        def place_table_scales(rows):
-            for r in rows:
+        def place_table_scales():
+            for r in range(4):
                 first = ROW_STEP * r
                 nc.sync.dma_start(
                     out=v_scale[r:P:32, :, :],
@@ -132,9 +132,8 @@ def tile_list_tabres_bias_kernel(
         load_down(0, 1)
         load_down(1, 1)
         nc.vector.tensor_copy(picked_scale[:], tab_scale[:].bitcast(U8).indirect(offsets[:]))
-        place_table_scales((0, 1))
         load_table(1)
-        place_table_scales((2, 3))
+        place_table_scales()
         load_down(2, 1)
         load_table(2)
         load_residual(RESIDUAL_LOADS[0])
@@ -195,7 +194,15 @@ def tile_list_tabres_bias_kernel(
 
 
         def gather_residual(c):
-            nc.vector.tensor_copy(result[c], r_rows[c].indirect(offsets[:]))
+            on_vector = [half for half in range(HALVES) if c * HALVES + half >= GPSIMD_BANKS]
+            if not on_vector:
+                nc.vector.tensor_copy(result[c], r_rows[c].indirect(offsets[:]))
+                return
+            for half in on_vector + [half for half in range(HALVES) if half not in on_vector]:
+                picked = result[c][:, half * BANK : (half + 1) * BANK]
+                nc.vector.tensor_copy(picked, r_rows[c].indirect(list_part(half * BANK, BANK)))
+                if half in on_vector:
+                    nc.scalar.activation(out=picked, in_=picked, func=IDENTITY, bias=bias[:, c : c + 1])
 
         gather_residual(0)
         h_words = keep.tile([P, S], U32, name="first_rows", align_bytes=64)
@@ -255,14 +262,7 @@ def tile_list_tabres_bias_kernel(
                     nc.scalar.activation(out=y_biased[:], in_=y_bank[:], func=IDENTITY, bias=bias[:, c : c + 1])
                     nc.gpsimd.tensor_tensor(out=result[c][:, cols], in0=y_biased[:], in1=result[c][:, cols], op=ADD)
                 else:
-                    nc.vector.scalar_tensor_tensor(
-                        out=result[c][:, cols],
-                        in0=y_bank[:],
-                        scalar=bias[:, c : c + 1],
-                        in1=result[c][:, cols],
-                        op0=ADD,
-                        op1=ADD,
-                    )
+                    nc.vector.tensor_tensor(out=result[c][:, cols], in0=y_bank[:], in1=result[c][:, cols], op=ADD)
             if c in stored:
                 count = store_size[c]
                 written = out[(c + 1 - count) * P : (c + 1) * P, :]

@@ -27,7 +27,7 @@ ROW_TILES = M // P
 H_COLS = BANK // PACK
 LIST_ROWS = 16
 UP_COLS = 256
-GPSIMD_BANKS = 13
+GPSIMD_TILES = 7
 SCALE_ROWS = 16
 ROW_STEP = 6
 PASS_STEP = 8
@@ -43,7 +43,7 @@ def tile_list_tabres_bias_kernel(
     nc = tc.nc
     with ExitStack() as ctx:
         keep = ctx.enter_context(tc.tile_pool(name="keep", bufs=1))
-        staged = ctx.enter_context(tc.tile_pool(name="staged", bufs=4))
+        staged = ctx.enter_context(tc.tile_pool(name="staged", bufs=2))
         psum = ctx.enter_context(tc.psum_pool(name="psum", bufs=8))
 
         offsets = keep.tile([P, S // LIST_ROWS], U16, name="offsets")
@@ -189,20 +189,24 @@ def tile_list_tabres_bias_kernel(
                     out=up_bf[:, PACK * n0 : PACK * (n0 + UP_COLS)].rearrange("p (c i j) -> p c j i", i=4, j=PACK),
                     in_=up_raw[:, :, u * BANK + n0 : u * BANK + n0 + UP_COLS].rearrange("p j (c i) -> p c j i", i=4),
                 )
-            cols = slice(u * BANK, (u + 1) * BANK)
-            nc.vector.quantize_mx(out=up_words[:, cols].bitcast(FP8X4), scales=up_scale[:, cols], in_=up_bf[:])
+            step = UP_COLS if u == 0 else BANK
+            for n0 in range(0, BANK, step):
+                cols = slice(u * BANK + n0, u * BANK + n0 + step)
+                nc.vector.quantize_mx(
+                    out=up_words[:, cols].bitcast(FP8X4),
+                    scales=up_scale[:, cols],
+                    in_=up_bf[:, PACK * n0 : PACK * (n0 + step)],
+                )
 
 
         def gather_residual(c):
-            on_vector = [half for half in range(HALVES) if c * HALVES + half >= GPSIMD_BANKS]
-            if not on_vector:
+            if c < GPSIMD_TILES:
                 nc.vector.tensor_copy(result[c], r_rows[c].indirect(offsets[:]))
                 return
-            for half in on_vector + [half for half in range(HALVES) if half not in on_vector]:
-                picked = result[c][:, half * BANK : (half + 1) * BANK]
-                nc.vector.tensor_copy(picked, r_rows[c].indirect(list_part(half * BANK, BANK)))
-                if half in on_vector:
-                    nc.scalar.activation(out=picked, in_=picked, func=IDENTITY, bias=bias[:, c : c + 1])
+            for j0 in range(0, S, BANK):
+                picked = result[c][:, j0 : j0 + BANK]
+                nc.vector.tensor_copy(picked, r_rows[c].indirect(list_part(j0, BANK)))
+                nc.scalar.activation(out=picked, in_=picked, func=IDENTITY, bias=bias[:, c : c + 1])
 
         gather_residual(0)
         h_words = keep.tile([P, S], U32, name="first_rows", align_bytes=64)
@@ -235,6 +239,8 @@ def tile_list_tabres_bias_kernel(
 
         def finish(c):
             rows = slice(c * P, (c + 1) * P)
+            if c < GPSIMD_TILES:
+                y_biased = staged.tile([P, S], F32, name="y_biased")
             for half in range(HALVES):
                 cols = slice(half * BANK, (half + 1) * BANK)
                 y_bank = psum.tile([P, BANK], F32, name="bank")
@@ -257,12 +263,12 @@ def tile_list_tabres_bias_kernel(
                     start=False,
                     stop=True,
                 )
-                if c * HALVES + half < GPSIMD_BANKS:
-                    y_biased = staged.tile([P, BANK], F32, name="y_biased")
-                    nc.scalar.activation(out=y_biased[:], in_=y_bank[:], func=IDENTITY, bias=bias[:, c : c + 1])
-                    nc.gpsimd.tensor_tensor(out=result[c][:, cols], in0=y_biased[:], in1=result[c][:, cols], op=ADD)
+                if c < GPSIMD_TILES:
+                    nc.scalar.activation(out=y_biased[:, cols], in_=y_bank[:], func=IDENTITY, bias=bias[:, c : c + 1])
                 else:
                     nc.vector.tensor_tensor(out=result[c][:, cols], in0=y_bank[:], in1=result[c][:, cols], op=ADD)
+            if c < GPSIMD_TILES:
+                nc.gpsimd.tensor_tensor(out=result[c], in0=y_biased[:], in1=result[c], op=ADD)
             if c in stored:
                 count = store_size[c]
                 written = out[(c + 1 - count) * P : (c + 1) * P, :]

@@ -33,6 +33,8 @@ ROW_STEP = 6
 PASS_STEP = 8
 RESIDUAL_LOADS = ((0,), (1,), (2,), (3,), (4,), (5,), (6,), (7,))
 STORES = ((0, 1, 2), (3, 4), (5,), (6,), (7,))
+HALVED_ADDS = (0, 6)
+HALVED_STORES = (6, 7)
 HEAD_COLS = T // 4
 LAST_GATHER = 256
 
@@ -265,11 +267,17 @@ def tile_list_tabres_bias_kernel(
                 )
                 if c < GPSIMD_TILES:
                     nc.scalar.activation(out=y_biased[:, cols], in_=y_bank[:], func=IDENTITY, bias=bias[:, c : c + 1])
+                    if c in HALVED_ADDS:
+                        nc.gpsimd.tensor_tensor(
+                            out=result[c][:, cols], in0=y_biased[:, cols], in1=result[c][:, cols], op=ADD
+                        )
                 else:
                     nc.vector.tensor_tensor(out=result[c][:, cols], in0=y_bank[:], in1=result[c][:, cols], op=ADD)
-            if c < GPSIMD_TILES:
+                if c in HALVED_STORES:
+                    nc.sync.dma_start(out=out[rows, cols], in_=result[c][:, cols])
+            if c < GPSIMD_TILES and c not in HALVED_ADDS:
                 nc.gpsimd.tensor_tensor(out=result[c], in0=y_biased[:], in1=result[c], op=ADD)
-            if c in stored:
+            if c in stored and c not in HALVED_STORES:
                 count = store_size[c]
                 written = out[(c + 1 - count) * P : (c + 1) * P, :]
                 nc.sync.dma_start(out=written.rearrange("(c p) j -> p c j", p=P), in_=stored[c][:])

@@ -206,9 +206,7 @@ def tile_list_tabres_bias_kernel(
                 nc.vector.tensor_copy(result[c], r_rows[c].indirect(offsets[:]))
                 return
             for j0 in range(0, S, BANK):
-                picked = result[c][:, j0 : j0 + BANK]
-                nc.vector.tensor_copy(picked, r_rows[c].indirect(list_part(j0, BANK)))
-                nc.scalar.activation(out=picked, in_=picked, func=IDENTITY, bias=bias[:, c : c + 1])
+                nc.vector.tensor_copy(result[c][:, j0 : j0 + BANK], r_rows[c].indirect(list_part(j0, BANK)))
 
         gather_residual(0)
         h_words = keep.tile([P, S], U32, name="first_rows", align_bytes=64)
@@ -272,8 +270,19 @@ def tile_list_tabres_bias_kernel(
                             out=result[c][:, cols], in0=y_biased[:, cols], in1=result[c][:, cols], op=ADD
                         )
                 else:
-                    nc.vector.tensor_tensor(out=result[c][:, cols], in0=y_bank[:], in1=result[c][:, cols], op=ADD)
-                if c in HALVED_STORES:
+                    step = BANK if half == 0 else BANK // 2
+                    for j0 in range(0, BANK, step):
+                        piece = slice(half * BANK + j0, half * BANK + j0 + step)
+                        nc.vector.scalar_tensor_tensor(
+                            out=result[c][:, piece],
+                            in0=y_bank[:, j0 : j0 + step],
+                            scalar=bias[:, c : c + 1],
+                            in1=result[c][:, piece],
+                            op0=ADD,
+                            op1=ADD,
+                        )
+                        nc.sync.dma_start(out=out[rows, piece], in_=result[c][:, piece])
+                if c in HALVED_STORES and c < GPSIMD_TILES:
                     nc.sync.dma_start(out=out[rows, cols], in_=result[c][:, cols])
             if c < GPSIMD_TILES and c not in HALVED_ADDS:
                 nc.gpsimd.tensor_tensor(out=result[c], in0=y_biased[:], in1=result[c], op=ADD)

@@ -27,13 +27,14 @@ ROW_TILES = M // P
 H_COLS = BANK // PACK
 LIST_ROWS = 16
 UP_COLS = 256
-GPSIMD_TILES = 7
+GATHER_PIECES = {6: (512, 512), 7: (512, 256, 256)}
+VECTOR_COLS = 256
 SCALE_ROWS = 16
 ROW_STEP = 6
 PASS_STEP = 8
 RESIDUAL_LOADS = ((0,), (1,), (2,), (3,), (4,), (5,), (6,), (7,))
 STORES = ((0, 1, 2), (3, 4), (5,), (6,), (7,))
-HALVED_ADDS = (0, 6)
+HALVED_ADDS = (0, 6, 7)
 HALVED_STORES = (6, 7)
 HEAD_COLS = T // 4
 LAST_GATHER = 256
@@ -45,7 +46,7 @@ def tile_list_tabres_bias_kernel(
     nc = tc.nc
     with ExitStack() as ctx:
         keep = ctx.enter_context(tc.tile_pool(name="keep", bufs=1))
-        staged = ctx.enter_context(tc.tile_pool(name="staged", bufs=2))
+        staged = ctx.enter_context(tc.tile_pool(name="staged", bufs=3))
         psum = ctx.enter_context(tc.psum_pool(name="psum", bufs=8))
 
         offsets = keep.tile([P, S // LIST_ROWS], U16, name="offsets")
@@ -201,12 +202,16 @@ def tile_list_tabres_bias_kernel(
                 )
 
 
+        def pieces(widths):
+            return [slice(sum(widths[:i]), sum(widths[: i + 1])) for i in range(len(widths))]
+
         def gather_residual(c):
-            if c < GPSIMD_TILES:
+            if c not in GATHER_PIECES:
                 nc.vector.tensor_copy(result[c], r_rows[c].indirect(offsets[:]))
                 return
-            for j0 in range(0, S, BANK):
-                nc.vector.tensor_copy(result[c][:, j0 : j0 + BANK], r_rows[c].indirect(list_part(j0, BANK)))
+            for cols in pieces(GATHER_PIECES[c]):
+                window = r_rows[c].indirect(list_part(cols.start, cols.stop - cols.start))
+                nc.vector.tensor_copy(result[c][:, cols], window)
 
         gather_residual(0)
         h_words = keep.tile([P, S], U32, name="first_rows", align_bytes=64)
@@ -239,8 +244,7 @@ def tile_list_tabres_bias_kernel(
 
         def finish(c):
             rows = slice(c * P, (c + 1) * P)
-            if c < GPSIMD_TILES:
-                y_biased = staged.tile([P, S], F32, name="y_biased")
+            y_biased = staged.tile([P, S], F32, name="y_biased")
             for half in range(HALVES):
                 cols = slice(half * BANK, (half + 1) * BANK)
                 y_bank = psum.tile([P, BANK], F32, name="bank")
@@ -263,28 +267,35 @@ def tile_list_tabres_bias_kernel(
                     start=False,
                     stop=True,
                 )
-                if c < GPSIMD_TILES:
-                    nc.scalar.activation(out=y_biased[:, cols], in_=y_bank[:], func=IDENTITY, bias=bias[:, c : c + 1])
-                    if c in HALVED_ADDS:
-                        nc.gpsimd.tensor_tensor(
-                            out=result[c][:, cols], in0=y_biased[:, cols], in1=result[c][:, cols], op=ADD
-                        )
-                else:
-                    step = BANK if half == 0 else BANK // 2
-                    for j0 in range(0, BANK, step):
-                        piece = slice(half * BANK + j0, half * BANK + j0 + step)
-                        nc.vector.scalar_tensor_tensor(
-                            out=result[c][:, piece],
-                            in0=y_bank[:, j0 : j0 + step],
-                            scalar=bias[:, c : c + 1],
-                            in1=result[c][:, piece],
-                            op0=ADD,
-                            op1=ADD,
-                        )
-                        nc.sync.dma_start(out=out[rows, piece], in_=result[c][:, piece])
-                if c in HALVED_STORES and c < GPSIMD_TILES:
-                    nc.sync.dma_start(out=out[rows, cols], in_=result[c][:, cols])
-            if c < GPSIMD_TILES and c not in HALVED_ADDS:
+                on_vector = VECTOR_COLS if (c, half) == (ROW_TILES - 1, HALVES - 1) else 0
+                staged_cols = slice(cols.start, cols.stop - on_vector)
+                nc.scalar.activation(
+                    out=y_biased[:, staged_cols],
+                    in_=y_bank[:, 0 : BANK - on_vector],
+                    func=IDENTITY,
+                    bias=bias[:, c : c + 1],
+                )
+                if c in HALVED_ADDS:
+                    nc.gpsimd.tensor_tensor(
+                        out=result[c][:, staged_cols],
+                        in0=y_biased[:, staged_cols],
+                        in1=result[c][:, staged_cols],
+                        op=ADD,
+                    )
+                if c in HALVED_STORES:
+                    nc.sync.dma_start(out=out[rows, staged_cols], in_=result[c][:, staged_cols])
+                if on_vector:
+                    piece = slice(staged_cols.stop, cols.stop)
+                    nc.vector.scalar_tensor_tensor(
+                        out=result[c][:, piece],
+                        in0=y_bank[:, BANK - on_vector : BANK],
+                        scalar=bias[:, c : c + 1],
+                        in1=result[c][:, piece],
+                        op0=ADD,
+                        op1=ADD,
+                    )
+                    nc.sync.dma_start(out=out[rows, piece], in_=result[c][:, piece])
+            if c not in HALVED_ADDS:
                 nc.gpsimd.tensor_tensor(out=result[c], in0=y_biased[:], in1=result[c], op=ADD)
             if c in stored and c not in HALVED_STORES:
                 count = store_size[c]

@@ -26,9 +26,11 @@ HALVES = S // BANK
 ROW_TILES = M // P
 H_COLS = BANK // PACK
 LIST_ROWS = 16
+GATHER_PIECES = {7: (512, 512)}
+LAST_ON_GPSIMD = 256
+VECTOR_PIECE = 256
+W4_HEAD = 4 * P
 UP_COLS = 256
-GATHER_PIECES = {6: (512, 512), 7: (512, 256, 256)}
-VECTOR_COLS = 256
 SCALE_ROWS = 16
 ROW_STEP = 6
 PASS_STEP = 8
@@ -93,7 +95,7 @@ def tile_list_tabres_bias_kernel(
         table = [keep.tile([P, T], I32, name="table%d" % a) for a in range(PASSES)]
         down_raw = {}
         up_raw = keep.tile([P, PACK, M], F32, name="up_raw")
-        w4 = keep.tile([P, PASSES, 2 * M], U8, name="w4", align_bytes=64)
+        w4 = {}
         r_rows = {}
 
         def load_table(a, first=0, last=T):
@@ -111,8 +113,11 @@ def tile_list_tabres_bias_kernel(
             nc.sync.dma_start(out=up_raw[:], in_=up.rearrange("(p j) n -> p j n", j=PACK))
 
         def load_w4(first, last):
-            words = w4_words[first:last].bitcast(I32).rearrange("a p n -> p a n")
-            nc.sync.dma_start(out=w4[:, first:last, :].bitcast(I32), in_=words)
+            part = keep.tile([P, PASSES, 2 * (last - first)], U8, name="w4_%d" % first, align_bytes=64)
+            words = w4_words[:, :, 2 * first : 2 * last].bitcast(I32).rearrange("a p n -> p a n")
+            nc.sync.dma_start(out=part[:].bitcast(I32), in_=words)
+            for c in range(first // P, last // P):
+                w4[c] = part[:, :, 2 * (c * P - first) : 2 * ((c + 1) * P - first)]
 
         buffer_of = {0: "first_rows", 1: "table0", 2: "down_raw0", 7: "table1"}
 
@@ -140,10 +145,9 @@ def tile_list_tabres_bias_kernel(
         load_down(2, 1)
         load_table(2)
         load_residual(RESIDUAL_LOADS[0])
-        load_w4_scales()
-        load_w4(0, 1)
         load_up()
-        load_w4(1, PASSES)
+        load_w4_scales()
+        load_w4(0, W4_HEAD)
 
         bias_t = psum.tile([P, P], F32, name="bank")
         nc.tensor.transpose(bias_t[:], b_rows[:], identity[:])
@@ -161,10 +165,13 @@ def tile_list_tabres_bias_kernel(
 
         def quantize_down(a):
             down_bf = keep.tile([P, PACK * R], BF16, name="down_bf%d" % a, align_bytes=64)
-            nc.scalar.copy(
-                out=down_bf[:].rearrange("p (t m j) -> p m j t", t=PACK, j=PACK),
-                in_=down_raw[a].rearrange("p (j m t) -> p m j t", j=PACK, t=PACK),
-            )
+            rounded = down_bf[:].rearrange("p (t m j) -> p m j t", t=PACK, j=PACK)
+            raw = down_raw[a].rearrange("p (j m t) -> p m j t", j=PACK, t=PACK)
+            if a == PASSES - 1:
+                nc.scalar.copy(out=rounded[:, :, :, 0:2], in_=raw[:, :, :, 0:2])
+                nc.vector.tensor_copy(out=rounded[:, :, :, 2:4], in_=raw[:, :, :, 2:4])
+            else:
+                nc.scalar.copy(out=rounded, in_=raw)
             nc.vector.quantize_mx(out=down_words[:, a, :].bitcast(FP8X4), scales=down_scale[:, a, :], in_=down_bf[:])
 
         gather_words(0, 0, S)
@@ -175,7 +182,10 @@ def tile_list_tabres_bias_kernel(
         for j0 in range(0, S, LAST_GATHER):
             gather_words(PASSES - 1, j0, LAST_GATHER)
 
-        for tiles in RESIDUAL_LOADS[1:]:
+        for tiles in RESIDUAL_LOADS[1:4]:
+            load_residual(tiles)
+        load_w4(W4_HEAD, M)
+        for tiles in RESIDUAL_LOADS[4:]:
             load_residual(tiles)
 
         store_size = {tiles[-1]: len(tiles) for tiles in STORES}
@@ -200,7 +210,6 @@ def tile_list_tabres_bias_kernel(
                     scales=up_scale[:, cols],
                     in_=up_bf[:, PACK * n0 : PACK * (n0 + step)],
                 )
-
 
         def pieces(widths):
             return [slice(sum(widths[:i]), sum(widths[: i + 1])) for i in range(len(widths))]
@@ -251,7 +260,7 @@ def tile_list_tabres_bias_kernel(
                 for a in range(PASSES):
                     nc.tensor.matmul_mx(
                         out=y_bank[:],
-                        lhsT=w4[:, a, 2 * c * P : 2 * (c + 1) * P].bitcast(FP4X4),
+                        lhsT=w4[c][:, a, :].bitcast(FP4X4),
                         lhsT_scale=w4_scale[:, a, :].bitcast(U8)[:, rows],
                         rhs=v_words[a][:, cols].bitcast(FP8X4),
                         rhs_scale=v_scale[:, a, :].bitcast(U8)[:, cols],
@@ -267,34 +276,36 @@ def tile_list_tabres_bias_kernel(
                     start=False,
                     stop=True,
                 )
-                on_vector = VECTOR_COLS if (c, half) == (ROW_TILES - 1, HALVES - 1) else 0
-                staged_cols = slice(cols.start, cols.stop - on_vector)
-                nc.scalar.activation(
-                    out=y_biased[:, staged_cols],
-                    in_=y_bank[:, 0 : BANK - on_vector],
-                    func=IDENTITY,
-                    bias=bias[:, c : c + 1],
-                )
-                if c in HALVED_ADDS:
-                    nc.gpsimd.tensor_tensor(
-                        out=result[c][:, staged_cols],
-                        in0=y_biased[:, staged_cols],
-                        in1=result[c][:, staged_cols],
-                        op=ADD,
+                staged_count = BANK if c < ROW_TILES - 1 else LAST_ON_GPSIMD * (half == 0)
+                staged_cols = slice(cols.start, cols.start + staged_count)
+                if staged_count:
+                    nc.scalar.activation(
+                        out=y_biased[:, staged_cols],
+                        in_=y_bank[:, 0:staged_count],
+                        func=IDENTITY,
+                        bias=bias[:, c : c + 1],
                     )
-                if c in HALVED_STORES:
-                    nc.sync.dma_start(out=out[rows, staged_cols], in_=result[c][:, staged_cols])
-                if on_vector:
-                    piece = slice(staged_cols.stop, cols.stop)
+                    if c in HALVED_ADDS:
+                        nc.gpsimd.tensor_tensor(
+                            out=result[c][:, staged_cols],
+                            in0=y_biased[:, staged_cols],
+                            in1=result[c][:, staged_cols],
+                            op=ADD,
+                        )
+                for j0 in range(staged_count, BANK, VECTOR_PIECE):
+                    piece = slice(cols.start + j0, cols.start + j0 + VECTOR_PIECE)
                     nc.vector.scalar_tensor_tensor(
                         out=result[c][:, piece],
-                        in0=y_bank[:, BANK - on_vector : BANK],
+                        in0=y_bank[:, j0 : j0 + VECTOR_PIECE],
                         scalar=bias[:, c : c + 1],
                         in1=result[c][:, piece],
                         op0=ADD,
                         op1=ADD,
                     )
-                    nc.sync.dma_start(out=out[rows, piece], in_=result[c][:, piece])
+                    if not staged_count:
+                        nc.sync.dma_start(out=out[rows, piece], in_=result[c][:, piece])
+                if c in HALVED_STORES and staged_count:
+                    nc.sync.dma_start(out=out[rows, cols], in_=result[c][:, cols])
             if c not in HALVED_ADDS:
                 nc.gpsimd.tensor_tensor(out=result[c], in0=y_biased[:], in1=result[c], op=ADD)
             if c in stored and c not in HALVED_STORES:

@@ -27,11 +27,12 @@ ROW_TILES = M // P
 H_COLS = BANK // PACK
 LIST_ROWS = 16
 GATHER_PIECES = {7: (512, 512)}
-LAST_ON_GPSIMD = 256
+LAST_ON_GPSIMD = 0
 VECTOR_PIECE = 256
 W4_HEAD = 4 * P
 UP_COLS = 256
 SCALE_ROWS = 16
+WARM_UPS = 2
 ROW_STEP = 6
 PASS_STEP = 8
 RESIDUAL_LOADS = ((0,), (1,), (2,), (3,), (4,), (5,), (6,), (7,))
@@ -250,6 +251,17 @@ def tile_list_tabres_bias_kernel(
         def quantize_h(half):
             cols = slice(half * BANK, (half + 1) * BANK)
             nc.vector.quantize_mx(out=h_words[:, cols].bitcast(FP8X4), scales=h_scale[:, cols], in_=h_bfs[half][:])
+            unread = psum.tile([P, BANK], F32, name="bank")
+            for i in range(WARM_UPS):
+                nc.tensor.matmul_mx(
+                    out=unread[:],
+                    lhsT=down_words[:, 0, 0:P].bitcast(FP8X4),
+                    lhsT_scale=down_scale[:, 0, 0:P],
+                    rhs=h_words[:, cols].bitcast(FP8X4),
+                    rhs_scale=h_scale[:, cols],
+                    start=True,
+                    stop=True,
+                )
 
         def finish(c):
             rows = slice(c * P, (c + 1) * P)
@@ -292,11 +304,12 @@ def tile_list_tabres_bias_kernel(
                             in1=result[c][:, staged_cols],
                             op=ADD,
                         )
-                for j0 in range(staged_count, BANK, VECTOR_PIECE):
-                    piece = slice(cols.start + j0, cols.start + j0 + VECTOR_PIECE)
+                step = VECTOR_PIECE if half else BANK
+                for j0 in range(staged_count, BANK, step):
+                    piece = slice(cols.start + j0, cols.start + j0 + step)
                     nc.vector.scalar_tensor_tensor(
                         out=result[c][:, piece],
-                        in0=y_bank[:, j0 : j0 + VECTOR_PIECE],
+                        in0=y_bank[:, j0 : j0 + step],
                         scalar=bias[:, c : c + 1],
                         in1=result[c][:, piece],
                         op0=ADD,

@@ -52,21 +52,21 @@ def tile_list_tabres_bias_kernel(
         staged = ctx.enter_context(tc.tile_pool(name="staged", bufs=3))
         psum = ctx.enter_context(tc.psum_pool(name="psum", bufs=8))
 
-        offsets = keep.tile([P, S // LIST_ROWS], U16, name="offsets")
+        offsets = keep.tile([P, S // LIST_ROWS], U16, name="offsets", align_bytes=256)
         nc.sync.dma_start(offsets[:], offs)
 
         def list_part(first, count):
             return offsets[:, first // LIST_ROWS : (first + count) // LIST_ROWS]
 
-        tab_scale = keep.tile([P, T // 4], I32, name="tab_scale", align_bytes=64)
+        tab_scale = keep.tile([P, T // 4], I32, name="tab_scale", align_bytes=256)
         nc.vector.memset(tab_scale[:], 0)
-        b_rows = keep.tile([P, P], F32, name="b_rows")
+        b_rows = keep.tile([P, P], F32, name="b_rows", align_bytes=256)
         nc.vector.memset(b_rows[:], 0.0)
-        v_scale = keep.tile([P, PASSES, S // 4], I32, name="v_scale", align_bytes=64)
-        w4_scale = keep.tile([P, PASSES, M // 4], I32, name="w4_scale", align_bytes=64)
+        v_scale = keep.tile([P, PASSES, S // 4], I32, name="v_scale", align_bytes=256)
+        w4_scale = keep.tile([P, PASSES, M // 4], I32, name="w4_scale", align_bytes=256)
         nc.vector.memset(v_scale[:], 0)
         nc.vector.memset(w4_scale[:], 0)
-        picked_scale = keep.tile([P, S], U8, name="picked_scale", align_bytes=64)
+        picked_scale = keep.tile([P, S], U8, name="picked_scale", align_bytes=256)
 
         def load_table_scales():
             for a in range(PASSES):
@@ -90,12 +90,12 @@ def tile_list_tabres_bias_kernel(
                     in_=w4_scales[:, r:16:4, :].bitcast(I32).rearrange("a q n -> q a n"),
                 )
 
-        identity = keep.tile([P, P], F32, name="identity")
+        identity = keep.tile([P, P], F32, name="identity", align_bytes=256)
         make_identity(nc, identity[:])
 
-        table = [keep.tile([P, T], I32, name="table%d" % a) for a in range(PASSES)]
+        table = [keep.tile([P, T], I32, name="table%d" % a, align_bytes=256) for a in range(PASSES)]
         down_raw = {}
-        up_raw = keep.tile([P, PACK, M], F32, name="up_raw")
+        up_raw = keep.tile([P, PACK, M], F32, name="up_raw", align_bytes=256)
         w4 = {}
         r_rows = {}
 
@@ -104,7 +104,7 @@ def tile_list_tabres_bias_kernel(
             nc.sync.dma_start(out=table[a][:, first:last], in_=words[:, first:last])
 
         def load_down(first, count):
-            raw = keep.tile([P, count, PACK * R], F32, name="down_raw%d" % first)
+            raw = keep.tile([P, count, PACK * R], F32, name="down_raw%d" % first, align_bytes=256)
             rows = down[first * K_PASS : (first + count) * K_PASS, :]
             nc.sync.dma_start(out=raw[:], in_=rows.rearrange("(a p j) r -> p a (j r)", p=P, j=PACK))
             for a in range(count):
@@ -114,7 +114,7 @@ def tile_list_tabres_bias_kernel(
             nc.sync.dma_start(out=up_raw[:], in_=up.rearrange("(p j) n -> p j n", j=PACK))
 
         def load_w4(first, last):
-            part = keep.tile([P, PASSES, 2 * (last - first)], U8, name="w4_%d" % first, align_bytes=64)
+            part = keep.tile([P, PASSES, 2 * (last - first)], U8, name="w4_%d" % first, align_bytes=256)
             words = w4_words[:, :, 2 * first : 2 * last].bitcast(I32).rearrange("a p n -> p a n")
             nc.sync.dma_start(out=part[:].bitcast(I32), in_=words)
             for c in range(first // P, last // P):
@@ -126,9 +126,9 @@ def tile_list_tabres_bias_kernel(
             first, count = tiles[0], len(tiles)
             name = buffer_of.get(first, "r_rows%d" % first)
             if first == 0:
-                raw = keep.tile([P, count, T], F32, name=name, align_bytes=64)
+                raw = keep.tile([P, count, T], F32, name=name, align_bytes=256)
             else:
-                raw = keep.tile([P, count, T], F32, name=name)
+                raw = keep.tile([P, count, T], F32, name=name, align_bytes=256)
             rows = rT[first * P : (first + count) * P, :]
             nc.sync.dma_start(out=raw[:], in_=rows.rearrange("(c p) t -> p c t", p=P))
             for c in range(count):
@@ -152,12 +152,12 @@ def tile_list_tabres_bias_kernel(
 
         bias_t = psum.tile([P, P], F32, name="bank")
         nc.tensor.transpose(bias_t[:], b_rows[:], identity[:])
-        bias = keep.tile([P, ROW_TILES], F32, name="bias")
+        bias = keep.tile([P, ROW_TILES], F32, name="bias", align_bytes=256)
         nc.scalar.activation(out=bias[:], in_=bias_t[:, 0:ROW_TILES], func=IDENTITY)
 
-        v_words = [keep.tile([P, S], U32, name="v_words%d" % a, align_bytes=64) for a in range(PASSES)]
-        down_words = keep.tile([P, PASSES, R], U32, name="down_words", align_bytes=64)
-        down_scale = keep.tile([P, PASSES, R], U8, name="down_scale", align_bytes=64)
+        v_words = [keep.tile([P, S], U32, name="v_words%d" % a, align_bytes=256) for a in range(PASSES)]
+        down_words = keep.tile([P, PASSES, R], U32, name="down_words", align_bytes=256)
+        down_scale = keep.tile([P, PASSES, R], U8, name="down_scale", align_bytes=256)
 
         def gather_words(a, j0, count):
             nc.vector.tensor_copy(
@@ -165,7 +165,7 @@ def tile_list_tabres_bias_kernel(
             )
 
         def quantize_down(a):
-            down_bf = keep.tile([P, PACK * R], BF16, name="down_bf%d" % a, align_bytes=64)
+            down_bf = keep.tile([P, PACK * R], BF16, name="down_bf%d" % a, align_bytes=256)
             rounded = down_bf[:].rearrange("p (t m j) -> p m j t", t=PACK, j=PACK)
             raw = down_raw[a].rearrange("p (j m t) -> p m j t", j=PACK, t=PACK)
             if a == PASSES - 1:
@@ -190,13 +190,13 @@ def tile_list_tabres_bias_kernel(
             load_residual(tiles)
 
         store_size = {tiles[-1]: len(tiles) for tiles in STORES}
-        stored = {tiles[-1]: keep.tile([P, len(tiles), S], F32, name="result%d" % tiles[0]) for tiles in STORES}
+        stored = {tiles[-1]: keep.tile([P, len(tiles), S], F32, name="result%d" % tiles[0], align_bytes=256) for tiles in STORES}
         result = {c: stored[tiles[-1]][:, c - tiles[0], :] for tiles in STORES for c in tiles}
-        up_words = keep.tile([P, M], U32, name="up_words", align_bytes=64)
-        up_scale = keep.tile([P, M], U8, name="up_scale", align_bytes=64)
+        up_words = keep.tile([P, M], U32, name="up_words", align_bytes=256)
+        up_scale = keep.tile([P, M], U8, name="up_scale", align_bytes=256)
 
         def quantize_up(u):
-            up_bf = keep.tile([P, PACK * BANK], BF16, name="up_bf%d" % u, align_bytes=64)
+            up_bf = keep.tile([P, PACK * BANK], BF16, name="up_bf%d" % u, align_bytes=256)
             cast = nc.vector.tensor_copy if u == 0 else nc.scalar.copy
             for n0 in range(0, BANK, UP_COLS):
                 cast(
@@ -224,9 +224,9 @@ def tile_list_tabres_bias_kernel(
                 nc.vector.tensor_copy(result[c][:, cols], window)
 
         gather_residual(0)
-        h_words = keep.tile([P, S], U32, name="first_rows", align_bytes=64)
-        h_scale = keep.tile([P, S], U8, name="h_scale", align_bytes=64)
-        h_bfs = [keep.tile([P, PACK * BANK], BF16, name="h_bf%d" % half, align_bytes=64) for half in range(HALVES)]
+        h_words = keep.tile([P, S], U32, name="first_rows", align_bytes=256)
+        h_scale = keep.tile([P, S], U8, name="h_scale", align_bytes=256)
+        h_bfs = [keep.tile([P, PACK * BANK], BF16, name="h_bf%d" % half, align_bytes=256) for half in range(HALVES)]
         h_banks = [psum.tile([P, PACK, H_COLS], F32, name="bank") for i in range(S // H_COLS)]
         for a in range(PASSES):
             for i, h_bank in enumerate(h_banks):
@@ -265,7 +265,7 @@ def tile_list_tabres_bias_kernel(
 
         def finish(c):
             rows = slice(c * P, (c + 1) * P)
-            y_biased = staged.tile([P, S], F32, name="y_biased")
+            y_biased = staged.tile([P, S], F32, name="y_biased", align_bytes=256)
             for half in range(HALVES):
                 cols = slice(half * BANK, (half + 1) * BANK)
                 y_bank = psum.tile([P, BANK], F32, name="bank")

@@ -26,18 +26,19 @@ HALVES = S // BANK
 ROW_TILES = M // P
 H_COLS = BANK // PACK
 LIST_ROWS = 16
-GATHER_PIECES = {7: (512, 512)}
-LAST_ON_GPSIMD = 0
+GATHER_PIECES = {c: (512, 512) for c in range(8)}
+LAST_ON_GPSIMD = 256
 VECTOR_PIECE = 256
 W4_HEAD = 4 * P
 UP_COLS = 256
 SCALE_ROWS = 16
-WARM_UPS = 2
+WARM_UPS = 4
 ROW_STEP = 6
 PASS_STEP = 8
 RESIDUAL_LOADS = ((0,), (1,), (2,), (3,), (4,), (5,), (6,), (7,))
 STORES = ((0, 1, 2), (3, 4), (5,), (6,), (7,))
-HALVED_ADDS = (0, 6, 7)
+HALVED_ADDS = tuple(range(8))
+H_ON_VECTOR = (4, 6)
 HALVED_STORES = (6, 7)
 HEAD_COLS = T // 4
 LAST_GATHER = 256
@@ -120,7 +121,7 @@ def tile_list_tabres_bias_kernel(
             for c in range(first // P, last // P):
                 w4[c] = part[:, :, 2 * (c * P - first) : 2 * ((c + 1) * P - first)]
 
-        buffer_of = {0: "first_rows", 1: "table0", 2: "down_raw0", 7: "table1"}
+        buffer_of = {0: "table0", 1: "down_raw0", 2: "down_raw1", 7: "table1"}
 
         def load_residual(tiles):
             first, count = tiles[0], len(tiles)
@@ -145,7 +146,6 @@ def tile_list_tabres_bias_kernel(
         place_table_scales()
         load_down(2, 1)
         load_table(2)
-        load_residual(RESIDUAL_LOADS[0])
         load_up()
         load_w4_scales()
         load_w4(0, W4_HEAD)
@@ -183,10 +183,10 @@ def tile_list_tabres_bias_kernel(
         for j0 in range(0, S, LAST_GATHER):
             gather_words(PASSES - 1, j0, LAST_GATHER)
 
-        for tiles in RESIDUAL_LOADS[1:4]:
+        for tiles in RESIDUAL_LOADS[0:3]:
             load_residual(tiles)
         load_w4(W4_HEAD, M)
-        for tiles in RESIDUAL_LOADS[4:]:
+        for tiles in RESIDUAL_LOADS[3:]:
             load_residual(tiles)
 
         store_size = {tiles[-1]: len(tiles) for tiles in STORES}
@@ -223,10 +223,20 @@ def tile_list_tabres_bias_kernel(
                 window = r_rows[c].indirect(list_part(cols.start, cols.stop - cols.start))
                 nc.vector.tensor_copy(result[c][:, cols], window)
 
-        gather_residual(0)
-        h_words = keep.tile([P, S], U32, name="first_rows", align_bytes=256)
+        h_words = keep.tile([P, S], U32, name="h_words", align_bytes=256)
         h_scale = keep.tile([P, S], U8, name="h_scale", align_bytes=256)
         h_bfs = [keep.tile([P, PACK * BANK], BF16, name="h_bf%d" % half, align_bytes=256) for half in range(HALVES)]
+        unread = psum.tile([P, BANK], F32, name="bank")
+        for i in range(WARM_UPS):
+            nc.tensor.matmul_mx(
+                out=unread[:],
+                lhsT=down_words[:, 0, 0:P].bitcast(FP8X4),
+                lhsT_scale=down_scale[:, 0, 0:P],
+                rhs=down_words[:, 0, :].bitcast(FP8X4),
+                rhs_scale=down_scale[:, 0, :],
+                start=True,
+                stop=True,
+            )
         h_banks = [psum.tile([P, PACK, H_COLS], F32, name="bank") for i in range(S // H_COLS)]
         for a in range(PASSES):
             for i, h_bank in enumerate(h_banks):
@@ -243,7 +253,7 @@ def tile_list_tabres_bias_kernel(
                     )
         for i, h_bank in enumerate(h_banks):
             half, part = divmod(i, PACK)
-            nc.scalar.copy(
+            (nc.vector.tensor_copy if i in H_ON_VECTOR else nc.scalar.copy)(
                 out=h_bfs[half][:, part * BANK : (part + 1) * BANK].rearrange("p (n t) -> p n t", t=PACK),
                 in_=h_bank[:].rearrange("p t n -> p n t"),
             )
@@ -251,17 +261,6 @@ def tile_list_tabres_bias_kernel(
         def quantize_h(half):
             cols = slice(half * BANK, (half + 1) * BANK)
             nc.vector.quantize_mx(out=h_words[:, cols].bitcast(FP8X4), scales=h_scale[:, cols], in_=h_bfs[half][:])
-            unread = psum.tile([P, BANK], F32, name="bank")
-            for i in range(WARM_UPS):
-                nc.tensor.matmul_mx(
-                    out=unread[:],
-                    lhsT=down_words[:, 0, 0:P].bitcast(FP8X4),
-                    lhsT_scale=down_scale[:, 0, 0:P],
-                    rhs=h_words[:, cols].bitcast(FP8X4),
-                    rhs_scale=h_scale[:, cols],
-                    start=True,
-                    stop=True,
-                )
 
         def finish(c):
             rows = slice(c * P, (c + 1) * P)
@@ -304,7 +303,7 @@ def tile_list_tabres_bias_kernel(
                             in1=result[c][:, staged_cols],
                             op=ADD,
                         )
-                step = VECTOR_PIECE if half else BANK
+                step = VECTOR_PIECE if half or staged_count else BANK
                 for j0 in range(staged_count, BANK, step):
                     piece = slice(cols.start + j0, cols.start + j0 + step)
                     nc.vector.scalar_tensor_tensor(
@@ -331,6 +330,5 @@ def tile_list_tabres_bias_kernel(
         quantize_up(0)
         quantize_up(1)
         for c in range(ROW_TILES):
-            if c + 1 < ROW_TILES:
-                gather_residual(c + 1)
+            gather_residual(c)
             finish(c)

@@ -38,7 +38,7 @@ PASS_STEP = 8
 RESIDUAL_LOADS = ((0,), (1,), (2,), (3,), (4,), (5,), (6,), (7,))
 STORES = ((0, 1, 2), (3, 4), (5,), (6,), (7,))
 HALVED_ADDS = tuple(range(8))
-H_ON_VECTOR = (4, 6)
+H_ON_VECTOR = (2, 3, 4)
 HALVED_STORES = (6, 7)
 HEAD_COLS = T // 4
 LAST_GATHER = 256
@@ -183,10 +183,10 @@ def tile_list_tabres_bias_kernel(
         for j0 in range(0, S, LAST_GATHER):
             gather_words(PASSES - 1, j0, LAST_GATHER)
 
-        for tiles in RESIDUAL_LOADS[0:3]:
+        for tiles in RESIDUAL_LOADS[0:4]:
             load_residual(tiles)
         load_w4(W4_HEAD, M)
-        for tiles in RESIDUAL_LOADS[3:]:
+        for tiles in RESIDUAL_LOADS[4:]:
             load_residual(tiles)
 
         store_size = {tiles[-1]: len(tiles) for tiles in STORES}

@@ -24,24 +24,24 @@ PASSES = K // K_PASS
 BANK = 512
 HALVES = S // BANK
 ROW_TILES = M // P
+LAST_TILE = ROW_TILES - 1
 H_COLS = BANK // PACK
 LIST_ROWS = 16
-GATHER_PIECES = {c: (512, 512) for c in range(8)}
-LAST_ON_GPSIMD = 256
-VECTOR_PIECE = 256
-W4_HEAD = 4 * P
-UP_COLS = 256
 SCALE_ROWS = 16
-WARM_UPS = 4
+QUADRANT = 32
+ROWS_IN_QUADRANT = 4
+ALIGN = 256
+
 ROW_STEP = 6
 PASS_STEP = 8
-RESIDUAL_LOADS = ((0,), (1,), (2,), (3,), (4,), (5,), (6,), (7,))
-STORES = ((0, 1, 2), (3, 4), (5,), (6,), (7,))
-HALVED_ADDS = tuple(range(8))
-H_ON_VECTOR = (2, 3, 4)
-HALVED_STORES = (6, 7)
-HEAD_COLS = T // 4
-LAST_GATHER = 256
+
+TABLE_HEAD = T // 4
+QUARTER = S // 4
+UP_PIECE = 256
+W4_HEAD_TILES = 4
+TILES_AHEAD_OF_W4_REST = 4
+H_BANKS_ON_VECTOR = (2, 3, 4)
+WHOLE_STORES = ((0, 1, 2), (3, 4), (5,))
 
 
 def tile_list_tabres_bias_kernel(
@@ -53,21 +53,24 @@ def tile_list_tabres_bias_kernel(
         staged = ctx.enter_context(tc.tile_pool(name="staged", bufs=3))
         psum = ctx.enter_context(tc.psum_pool(name="psum", bufs=8))
 
-        offsets = keep.tile([P, S // LIST_ROWS], U16, name="offsets", align_bytes=256)
+        def held(shape, dtype, name):
+            return keep.tile(shape, dtype, name=name, align_bytes=ALIGN)
+
+        offsets = held([P, S // LIST_ROWS], U16, "offsets")
         nc.sync.dma_start(offsets[:], offs)
 
-        def list_part(first, count):
-            return offsets[:, first // LIST_ROWS : (first + count) // LIST_ROWS]
+        def list_part(cols):
+            return offsets[:, cols.start // LIST_ROWS : cols.stop // LIST_ROWS]
 
-        tab_scale = keep.tile([P, T // 4], I32, name="tab_scale", align_bytes=256)
+        tab_scale = held([P, T // 4], I32, "tab_scale")
         nc.vector.memset(tab_scale[:], 0)
-        b_rows = keep.tile([P, P], F32, name="b_rows", align_bytes=256)
+        b_rows = held([P, P], F32, "b_rows")
         nc.vector.memset(b_rows[:], 0.0)
-        v_scale = keep.tile([P, PASSES, S // 4], I32, name="v_scale", align_bytes=256)
-        w4_scale = keep.tile([P, PASSES, M // 4], I32, name="w4_scale", align_bytes=256)
+        v_scale = held([P, PASSES, S // 4], I32, "v_scale")
+        w4_scale = held([P, PASSES, M // 4], I32, "w4_scale")
         nc.vector.memset(v_scale[:], 0)
         nc.vector.memset(w4_scale[:], 0)
-        picked_scale = keep.tile([P, S], U8, name="picked_scale", align_bytes=256)
+        picked_scale = held([P, S], U8, "picked_scale")
 
         def load_table_scales():
             for a in range(PASSES):
@@ -77,95 +80,82 @@ def tile_list_tabres_bias_kernel(
                 )
 
         def place_table_scales():
-            for r in range(4):
+            for r in range(ROWS_IN_QUADRANT):
                 first = ROW_STEP * r
+                last = first + PASS_STEP * (P // QUADRANT) * PASSES
                 nc.sync.dma_start(
-                    out=v_scale[r:P:32, :, :],
-                    in_=picked_scale[first : first + PASS_STEP * 4 * PASSES : PASS_STEP, :].bitcast(I32),
+                    out=v_scale[r:P:QUADRANT, :, :], in_=picked_scale[first:last:PASS_STEP, :].bitcast(I32)
                 )
 
         def load_w4_scales():
-            for r in range(4):
+            for r in range(ROWS_IN_QUADRANT):
                 nc.sync.dma_start(
-                    out=w4_scale[r:P:32, :, :],
-                    in_=w4_scales[:, r:16:4, :].bitcast(I32).rearrange("a q n -> q a n"),
+                    out=w4_scale[r:P:QUADRANT, :, :],
+                    in_=w4_scales[:, r:SCALE_ROWS:ROWS_IN_QUADRANT, :].bitcast(I32).rearrange("a q n -> q a n"),
                 )
 
-        identity = keep.tile([P, P], F32, name="identity", align_bytes=256)
+        identity = held([P, P], F32, "identity")
         make_identity(nc, identity[:])
 
-        table = [keep.tile([P, T], I32, name="table%d" % a, align_bytes=256) for a in range(PASSES)]
+        table = [held([P, T], I32, "table%d" % a) for a in range(PASSES)]
         down_raw = {}
-        up_raw = keep.tile([P, PACK, M], F32, name="up_raw", align_bytes=256)
+        up_raw = held([P, PACK, M], F32, "up_raw")
         w4 = {}
-        r_rows = {}
+        residual = {}
 
         def load_table(a, first=0, last=T):
             words = tab_words[a].rearrange("p t i -> p (t i)").bitcast(I32)
             nc.sync.dma_start(out=table[a][:, first:last], in_=words[:, first:last])
 
-        def load_down(first, count):
-            raw = keep.tile([P, count, PACK * R], F32, name="down_raw%d" % first, align_bytes=256)
-            rows = down[first * K_PASS : (first + count) * K_PASS, :]
+        def load_down(a):
+            raw = held([P, 1, PACK * R], F32, "down_raw%d" % a)
+            rows = down[a * K_PASS : (a + 1) * K_PASS, :]
             nc.sync.dma_start(out=raw[:], in_=rows.rearrange("(a p j) r -> p a (j r)", p=P, j=PACK))
-            for a in range(count):
-                down_raw[first + a] = raw[:, a, :]
-
-        def load_up():
-            nc.sync.dma_start(out=up_raw[:], in_=up.rearrange("(p j) n -> p j n", j=PACK))
+            down_raw[a] = raw[:, 0, :]
 
         def load_w4(first, last):
-            part = keep.tile([P, PASSES, 2 * (last - first)], U8, name="w4_%d" % first, align_bytes=256)
-            words = w4_words[:, :, 2 * first : 2 * last].bitcast(I32).rearrange("a p n -> p a n")
+            part = held([P, PASSES, 2 * P * (last - first)], U8, "w4_%d" % first)
+            words = w4_words[:, :, 2 * P * first : 2 * P * last].bitcast(I32).rearrange("a p n -> p a n")
             nc.sync.dma_start(out=part[:].bitcast(I32), in_=words)
-            for c in range(first // P, last // P):
-                w4[c] = part[:, :, 2 * (c * P - first) : 2 * ((c + 1) * P - first)]
+            for c in range(first, last):
+                w4[c] = part[:, :, 2 * P * (c - first) : 2 * P * (c + 1 - first)]
 
-        buffer_of = {0: "table0", 1: "down_raw0", 2: "down_raw1", 7: "table1"}
+        buffer_of = {0: "table0", 1: "down_raw0", 2: "down_raw1", LAST_TILE: "table1"}
 
-        def load_residual(tiles):
-            first, count = tiles[0], len(tiles)
-            name = buffer_of.get(first, "r_rows%d" % first)
-            if first == 0:
-                raw = keep.tile([P, count, T], F32, name=name, align_bytes=256)
-            else:
-                raw = keep.tile([P, count, T], F32, name=name, align_bytes=256)
-            rows = rT[first * P : (first + count) * P, :]
-            nc.sync.dma_start(out=raw[:], in_=rows.rearrange("(c p) t -> p c t", p=P))
-            for c in range(count):
-                r_rows[first + c] = raw[:, c, :]
+        def load_residual(c):
+            raw = held([P, 1, T], F32, buffer_of.get(c, "residual%d" % c))
+            nc.sync.dma_start(out=raw[:], in_=rT[c * P : (c + 1) * P, :].rearrange("(c p) t -> p c t", p=P))
+            residual[c] = raw[:, 0, :]
 
-        load_table(0, 0, HEAD_COLS)
+        load_table(0, 0, TABLE_HEAD)
         load_table_scales()
-        load_table(0, HEAD_COLS, T)
+        load_table(0, TABLE_HEAD, T)
         nc.sync.dma_start(out=b_rows[0:ROW_TILES, :], in_=b.rearrange("(c p) -> c p", p=P))
-        load_down(0, 1)
-        load_down(1, 1)
+        load_down(0)
+        load_down(1)
         nc.vector.tensor_copy(picked_scale[:], tab_scale[:].bitcast(U8).indirect(offsets[:]))
         load_table(1)
         place_table_scales()
-        load_down(2, 1)
+        load_down(2)
         load_table(2)
-        load_up()
+        nc.sync.dma_start(out=up_raw[:], in_=up.rearrange("(p j) n -> p j n", j=PACK))
         load_w4_scales()
-        load_w4(0, W4_HEAD)
+        load_w4(0, W4_HEAD_TILES)
 
-        bias_t = psum.tile([P, P], F32, name="bank")
-        nc.tensor.transpose(bias_t[:], b_rows[:], identity[:])
-        bias = keep.tile([P, ROW_TILES], F32, name="bias", align_bytes=256)
-        nc.scalar.activation(out=bias[:], in_=bias_t[:, 0:ROW_TILES], func=IDENTITY)
+        bias_bank = psum.tile([P, P], F32, name="bank")
+        nc.tensor.transpose(bias_bank[:], b_rows[:], identity[:])
+        bias = held([P, ROW_TILES], F32, "bias")
+        nc.scalar.activation(out=bias[:], in_=bias_bank[:, 0:ROW_TILES], func=IDENTITY)
 
-        v_words = [keep.tile([P, S], U32, name="v_words%d" % a, align_bytes=256) for a in range(PASSES)]
-        down_words = keep.tile([P, PASSES, R], U32, name="down_words", align_bytes=256)
-        down_scale = keep.tile([P, PASSES, R], U8, name="down_scale", align_bytes=256)
+        v_words = [held([P, S], U32, "v_words%d" % a) for a in range(PASSES)]
+        down_words = held([P, PASSES, R], U32, "down_words")
+        down_scale = held([P, PASSES, R], U8, "down_scale")
 
-        def gather_words(a, j0, count):
-            nc.vector.tensor_copy(
-                v_words[a][:, j0 : j0 + count], table[a][:].bitcast(U32).indirect(list_part(j0, count))
-            )
+        def gather_words(a, cols):
+            nc.vector.tensor_copy(v_words[a][:, cols], table[a][:].bitcast(U32).indirect(list_part(cols)))
 
         def quantize_down(a):
-            down_bf = keep.tile([P, PACK * R], BF16, name="down_bf%d" % a, align_bytes=256)
+            down_bf = held([P, PACK * R], BF16, "down_bf%d" % a)
             rounded = down_bf[:].rearrange("p (t m j) -> p m j t", t=PACK, j=PACK)
             raw = down_raw[a].rearrange("p (j m t) -> p m j t", j=PACK, t=PACK)
             if a == PASSES - 1:
@@ -175,68 +165,47 @@ def tile_list_tabres_bias_kernel(
                 nc.scalar.copy(out=rounded, in_=raw)
             nc.vector.quantize_mx(out=down_words[:, a, :].bitcast(FP8X4), scales=down_scale[:, a, :], in_=down_bf[:])
 
-        gather_words(0, 0, S)
+        gather_words(0, slice(0, S))
         quantize_down(0)
         quantize_down(1)
-        gather_words(1, 0, S)
+        gather_words(1, slice(0, S))
         quantize_down(2)
-        for j0 in range(0, S, LAST_GATHER):
-            gather_words(PASSES - 1, j0, LAST_GATHER)
+        for j in range(0, S, QUARTER):
+            gather_words(PASSES - 1, slice(j, j + QUARTER))
 
-        for tiles in RESIDUAL_LOADS[0:4]:
-            load_residual(tiles)
-        load_w4(W4_HEAD, M)
-        for tiles in RESIDUAL_LOADS[4:]:
-            load_residual(tiles)
+        for c in range(TILES_AHEAD_OF_W4_REST):
+            load_residual(c)
+        load_w4(W4_HEAD_TILES, ROW_TILES)
+        for c in range(TILES_AHEAD_OF_W4_REST, ROW_TILES):
+            load_residual(c)
 
-        store_size = {tiles[-1]: len(tiles) for tiles in STORES}
-        stored = {tiles[-1]: keep.tile([P, len(tiles), S], F32, name="result%d" % tiles[0], align_bytes=256) for tiles in STORES}
-        result = {c: stored[tiles[-1]][:, c - tiles[0], :] for tiles in STORES for c in tiles}
-        up_words = keep.tile([P, M], U32, name="up_words", align_bytes=256)
-        up_scale = keep.tile([P, M], U8, name="up_scale", align_bytes=256)
+        groups = WHOLE_STORES + tuple((c,) for c in range(WHOLE_STORES[-1][-1] + 1, ROW_TILES))
+        group_tile = {tiles: held([P, len(tiles), S], F32, "result%d" % tiles[0]) for tiles in groups}
+        result = {c: group_tile[tiles][:, c - tiles[0], :] for tiles in groups for c in tiles}
+        up_words = held([P, M], U32, "up_words")
+        up_scale = held([P, M], U8, "up_scale")
 
-        def quantize_up(u):
-            up_bf = keep.tile([P, PACK * BANK], BF16, name="up_bf%d" % u, align_bytes=256)
-            cast = nc.vector.tensor_copy if u == 0 else nc.scalar.copy
-            for n0 in range(0, BANK, UP_COLS):
-                cast(
-                    out=up_bf[:, PACK * n0 : PACK * (n0 + UP_COLS)].rearrange("p (c i j) -> p c j i", i=4, j=PACK),
-                    in_=up_raw[:, :, u * BANK + n0 : u * BANK + n0 + UP_COLS].rearrange("p j (c i) -> p c j i", i=4),
+        def quantize_up(half):
+            up_bf = held([P, PACK * BANK], BF16, "up_bf%d" % half)
+            round_copy = nc.vector.tensor_copy if half == 0 else nc.scalar.copy
+            first = half * BANK
+            for n in range(0, BANK, UP_PIECE):
+                round_copy(
+                    out=up_bf[:, PACK * n : PACK * (n + UP_PIECE)].rearrange("p (c i j) -> p c j i", i=4, j=PACK),
+                    in_=up_raw[:, :, first + n : first + n + UP_PIECE].rearrange("p j (c i) -> p c j i", i=4),
                 )
-            step = UP_COLS if u == 0 else BANK
-            for n0 in range(0, BANK, step):
-                cols = slice(u * BANK + n0, u * BANK + n0 + step)
+            step = UP_PIECE if half == 0 else BANK
+            for n in range(0, BANK, step):
+                cols = slice(first + n, first + n + step)
                 nc.vector.quantize_mx(
                     out=up_words[:, cols].bitcast(FP8X4),
                     scales=up_scale[:, cols],
-                    in_=up_bf[:, PACK * n0 : PACK * (n0 + step)],
+                    in_=up_bf[:, PACK * n : PACK * (n + step)],
                 )
 
-        def pieces(widths):
-            return [slice(sum(widths[:i]), sum(widths[: i + 1])) for i in range(len(widths))]
-
-        def gather_residual(c):
-            if c not in GATHER_PIECES:
-                nc.vector.tensor_copy(result[c], r_rows[c].indirect(offsets[:]))
-                return
-            for cols in pieces(GATHER_PIECES[c]):
-                window = r_rows[c].indirect(list_part(cols.start, cols.stop - cols.start))
-                nc.vector.tensor_copy(result[c][:, cols], window)
-
-        h_words = keep.tile([P, S], U32, name="h_words", align_bytes=256)
-        h_scale = keep.tile([P, S], U8, name="h_scale", align_bytes=256)
-        h_bfs = [keep.tile([P, PACK * BANK], BF16, name="h_bf%d" % half, align_bytes=256) for half in range(HALVES)]
-        unread = psum.tile([P, BANK], F32, name="bank")
-        for i in range(WARM_UPS):
-            nc.tensor.matmul_mx(
-                out=unread[:],
-                lhsT=down_words[:, 0, 0:P].bitcast(FP8X4),
-                lhsT_scale=down_scale[:, 0, 0:P],
-                rhs=down_words[:, 0, :].bitcast(FP8X4),
-                rhs_scale=down_scale[:, 0, :],
-                start=True,
-                stop=True,
-            )
+        h_words = held([P, S], U32, "h_words")
+        h_scale = held([P, S], U8, "h_scale")
+        h_bf = [held([P, PACK * BANK], BF16, "h_bf%d" % half) for half in range(HALVES)]
         h_banks = [psum.tile([P, PACK, H_COLS], F32, name="bank") for i in range(S // H_COLS)]
         for a in range(PASSES):
             for i, h_bank in enumerate(h_banks):
@@ -253,82 +222,80 @@ def tile_list_tabres_bias_kernel(
                     )
         for i, h_bank in enumerate(h_banks):
             half, part = divmod(i, PACK)
-            (nc.vector.tensor_copy if i in H_ON_VECTOR else nc.scalar.copy)(
-                out=h_bfs[half][:, part * BANK : (part + 1) * BANK].rearrange("p (n t) -> p n t", t=PACK),
+            round_copy = nc.vector.tensor_copy if i in H_BANKS_ON_VECTOR else nc.scalar.copy
+            round_copy(
+                out=h_bf[half][:, part * BANK : (part + 1) * BANK].rearrange("p (n t) -> p n t", t=PACK),
                 in_=h_bank[:].rearrange("p t n -> p n t"),
             )
-
-        def quantize_h(half):
+        for half in range(HALVES):
             cols = slice(half * BANK, (half + 1) * BANK)
-            nc.vector.quantize_mx(out=h_words[:, cols].bitcast(FP8X4), scales=h_scale[:, cols], in_=h_bfs[half][:])
+            nc.vector.quantize_mx(out=h_words[:, cols].bitcast(FP8X4), scales=h_scale[:, cols], in_=h_bf[half][:])
+        for half in range(HALVES):
+            quantize_up(half)
 
-        def finish(c):
+        def sum_y(c, cols):
             rows = slice(c * P, (c + 1) * P)
-            y_biased = staged.tile([P, S], F32, name="y_biased", align_bytes=256)
-            for half in range(HALVES):
-                cols = slice(half * BANK, (half + 1) * BANK)
-                y_bank = psum.tile([P, BANK], F32, name="bank")
-                for a in range(PASSES):
-                    nc.tensor.matmul_mx(
-                        out=y_bank[:],
-                        lhsT=w4[c][:, a, :].bitcast(FP4X4),
-                        lhsT_scale=w4_scale[:, a, :].bitcast(U8)[:, rows],
-                        rhs=v_words[a][:, cols].bitcast(FP8X4),
-                        rhs_scale=v_scale[:, a, :].bitcast(U8)[:, cols],
-                        start=(a == 0),
-                        stop=False,
-                    )
+            y_bank = psum.tile([P, BANK], F32, name="bank")
+            for a in range(PASSES):
                 nc.tensor.matmul_mx(
                     out=y_bank[:],
-                    lhsT=up_words[:, rows].bitcast(FP8X4),
-                    lhsT_scale=up_scale[:, rows],
-                    rhs=h_words[:, cols].bitcast(FP8X4),
-                    rhs_scale=h_scale[:, cols],
-                    start=False,
-                    stop=True,
+                    lhsT=w4[c][:, a, :].bitcast(FP4X4),
+                    lhsT_scale=w4_scale[:, a, :].bitcast(U8)[:, rows],
+                    rhs=v_words[a][:, cols].bitcast(FP8X4),
+                    rhs_scale=v_scale[:, a, :].bitcast(U8)[:, cols],
+                    start=(a == 0),
+                    stop=False,
                 )
-                staged_count = BANK if c < ROW_TILES - 1 else LAST_ON_GPSIMD * (half == 0)
-                staged_cols = slice(cols.start, cols.start + staged_count)
-                if staged_count:
+            nc.tensor.matmul_mx(
+                out=y_bank[:],
+                lhsT=up_words[:, rows].bitcast(FP8X4),
+                lhsT_scale=up_scale[:, rows],
+                rhs=h_words[:, cols].bitcast(FP8X4),
+                rhs_scale=h_scale[:, cols],
+                start=False,
+                stop=True,
+            )
+            return y_bank
+
+        def gather_residual(into, c, cols):
+            nc.vector.tensor_copy(into, residual[c].indirect(list_part(cols)))
+
+        halves = [slice(half * BANK, (half + 1) * BANK) for half in range(HALVES)]
+        group_ending_at = {tiles[-1]: tiles for tiles in WHOLE_STORES}
+        for c in range(ROW_TILES):
+            rows = slice(c * P, (c + 1) * P)
+            for cols in halves:
+                gather_residual(result[c][:, cols], c, cols)
+            y_biased = staged.tile([P, S], F32, name="y_biased", align_bytes=ALIGN)
+            for cols in halves:
+                y_bank = sum_y(c, cols)
+                split = cols.stop if c < LAST_TILE else max(cols.start, QUARTER)
+                if split > cols.start:
+                    part = slice(cols.start, split)
                     nc.scalar.activation(
-                        out=y_biased[:, staged_cols],
-                        in_=y_bank[:, 0:staged_count],
+                        out=y_biased[:, part],
+                        in_=y_bank[:, 0 : split - cols.start],
                         func=IDENTITY,
                         bias=bias[:, c : c + 1],
                     )
-                    if c in HALVED_ADDS:
-                        nc.gpsimd.tensor_tensor(
-                            out=result[c][:, staged_cols],
-                            in0=y_biased[:, staged_cols],
-                            in1=result[c][:, staged_cols],
-                            op=ADD,
-                        )
-                step = VECTOR_PIECE if half or staged_count else BANK
-                for j0 in range(staged_count, BANK, step):
-                    piece = slice(cols.start + j0, cols.start + j0 + step)
+                    nc.gpsimd.tensor_tensor(
+                        out=result[c][:, part], in0=y_biased[:, part], in1=result[c][:, part], op=ADD
+                    )
+                for j in range(split, cols.stop, QUARTER):
+                    part = slice(j, j + QUARTER)
                     nc.vector.scalar_tensor_tensor(
-                        out=result[c][:, piece],
-                        in0=y_bank[:, j0 : j0 + step],
+                        out=result[c][:, part],
+                        in0=y_bank[:, j - cols.start : j - cols.start + QUARTER],
                         scalar=bias[:, c : c + 1],
-                        in1=result[c][:, piece],
+                        in1=result[c][:, part],
                         op0=ADD,
                         op1=ADD,
                     )
-                    if not staged_count:
-                        nc.sync.dma_start(out=out[rows, piece], in_=result[c][:, piece])
-                if c in HALVED_STORES and staged_count:
+                    if split == cols.start:
+                        nc.sync.dma_start(out=out[rows, part], in_=result[c][:, part])
+                if c > WHOLE_STORES[-1][-1] and split > cols.start:
                     nc.sync.dma_start(out=out[rows, cols], in_=result[c][:, cols])
-            if c not in HALVED_ADDS:
-                nc.gpsimd.tensor_tensor(out=result[c], in0=y_biased[:], in1=result[c], op=ADD)
-            if c in stored and c not in HALVED_STORES:
-                count = store_size[c]
-                written = out[(c + 1 - count) * P : (c + 1) * P, :]
-                nc.sync.dma_start(out=written.rearrange("(c p) j -> p c j", p=P), in_=stored[c][:])
-
-        quantize_h(0)
-        quantize_h(1)
-        quantize_up(0)
-        quantize_up(1)
-        for c in range(ROW_TILES):
-            gather_residual(c)
-            finish(c)
+            if c in group_ending_at:
+                tiles = group_ending_at[c]
+                written = out[tiles[0] * P : (c + 1) * P, :]
+                nc.sync.dma_start(out=written.rearrange("(c p) j -> p c j", p=P), in_=group_tile[tiles][:])

@@ -38,6 +38,7 @@ PASS_STEP = 8
 TABLE_HEAD = T // 4
 QUARTER = S // 4
 UP_PIECE = 256
+W4_FIRST_TILES = 2
 W4_HEAD_TILES = 4
 TILES_AHEAD_OF_W4_REST = 4
 H_BANKS_ON_VECTOR = (2, 3, 4)
@@ -140,7 +141,7 @@ def tile_list_tabres_bias_kernel(
         load_table(2)
         nc.sync.dma_start(out=up_raw[:], in_=up.rearrange("(p j) n -> p j n", j=PACK))
         load_w4_scales()
-        load_w4(0, W4_HEAD_TILES)
+        load_w4(0, W4_FIRST_TILES)
 
         bias_bank = psum.tile([P, P], F32, name="bank")
         nc.tensor.transpose(bias_bank[:], b_rows[:], identity[:])
@@ -173,7 +174,9 @@ def tile_list_tabres_bias_kernel(
         for j in range(0, S, QUARTER):
             gather_words(PASSES - 1, slice(j, j + QUARTER))
 
-        for c in range(TILES_AHEAD_OF_W4_REST):
+        load_residual(0)
+        load_w4(W4_FIRST_TILES, W4_HEAD_TILES)
+        for c in range(1, TILES_AHEAD_OF_W4_REST):
             load_residual(c)
         load_w4(W4_HEAD_TILES, ROW_TILES)
         for c in range(TILES_AHEAD_OF_W4_REST, ROW_TILES):

from contextlib import ExitStack

import concourse.mybir as mybir
from concourse.masks import make_identity

K, M, T, S, R = 1536, 1024, 2048, 1024, 512
FLOPS = 2 * S * (K * R + K * M + R * M)

F32 = mybir.dt.float32
BF16 = mybir.dt.bfloat16
I32 = mybir.dt.int32
U32 = mybir.dt.uint32
U16 = mybir.dt.uint16
U8 = mybir.dt.uint8
FP8X4 = mybir.dt.float8_e4m3fn_x4
FP4X4 = mybir.dt.float4_e2m1fn_x4
ADD = mybir.AluOpType.add
IDENTITY = mybir.ActivationFunctionType.Identity

P = 128
PACK = 4
K_PASS = P * PACK
PASSES = K // K_PASS
BANK = 512
HALVES = S // BANK
ROW_TILES = M // P
LAST_TILE = ROW_TILES - 1
H_COLS = BANK // PACK
LIST_ROWS = 16
SCALE_ROWS = 16
QUADRANT = 32
ROWS_IN_QUADRANT = 4
ALIGN = 256

ROW_STEP = 6
PASS_STEP = 8

TABLE_HEAD = T // 4
QUARTER = S // 4
UP_PIECE = 256
W4_FIRST_TILES = 2
W4_HEAD_TILES = 4
TILES_AHEAD_OF_W4_REST = 4
H_BANKS_ON_VECTOR = (2, 3, 4)
WHOLE_STORES = ((0, 1, 2), (3, 4), (5,))


def tile_list_tabres_bias_kernel(
    tc, tab_words, tab_scales, w4_words, w4_scales, down, up, rT, b, offs, out
):
    nc = tc.nc
    with ExitStack() as ctx:
        keep = ctx.enter_context(tc.tile_pool(name="keep", bufs=1))
        staged = ctx.enter_context(tc.tile_pool(name="staged", bufs=3))
        psum = ctx.enter_context(tc.psum_pool(name="psum", bufs=8))

        def held(shape, dtype, name):
            return keep.tile(shape, dtype, name=name, align_bytes=ALIGN)

        offsets = held([P, S // LIST_ROWS], U16, "offsets")
        nc.sync.dma_start(offsets[:], offs)

        def list_part(cols):
            return offsets[:, cols.start // LIST_ROWS : cols.stop // LIST_ROWS]

        tab_scale = held([P, T // 4], I32, "tab_scale")
        nc.vector.memset(tab_scale[:], 0)
        b_rows = held([P, P], F32, "b_rows")
        nc.vector.memset(b_rows[:], 0.0)
        v_scale = held([P, PASSES, S // 4], I32, "v_scale")
        w4_scale = held([P, PASSES, M // 4], I32, "w4_scale")
        nc.vector.memset(v_scale[:], 0)
        nc.vector.memset(w4_scale[:], 0)
        picked_scale = held([P, S], U8, "picked_scale")

        def load_table_scales():
            for a in range(PASSES):
                first = PASS_STEP * a
                nc.sync.dma_start(
                    out=tab_scale[first : first + ROW_STEP * SCALE_ROWS : ROW_STEP, :], in_=tab_scales[a].bitcast(I32)
                )

        def place_table_scales():
            for r in range(ROWS_IN_QUADRANT):
                first = ROW_STEP * r
                last = first + PASS_STEP * (P // QUADRANT) * PASSES
                nc.sync.dma_start(
                    out=v_scale[r:P:QUADRANT, :, :], in_=picked_scale[first:last:PASS_STEP, :].bitcast(I32)
                )

        def load_w4_scales():
            for r in range(ROWS_IN_QUADRANT):
                nc.sync.dma_start(
                    out=w4_scale[r:P:QUADRANT, :, :],
                    in_=w4_scales[:, r:SCALE_ROWS:ROWS_IN_QUADRANT, :].bitcast(I32).rearrange("a q n -> q a n"),
                )

        identity = held([P, P], F32, "identity")
        make_identity(nc, identity[:])

        table = [held([P, T], I32, "table%d" % a) for a in range(PASSES)]
        down_raw = {}
        up_raw = held([P, PACK, M], F32, "up_raw")
        w4 = {}
        residual = {}

        def load_table(a, first=0, last=T):
            words = tab_words[a].rearrange("p t i -> p (t i)").bitcast(I32)
            nc.sync.dma_start(out=table[a][:, first:last], in_=words[:, first:last])

        def load_down(a):
            raw = held([P, 1, PACK * R], F32, "down_raw%d" % a)
            rows = down[a * K_PASS : (a + 1) * K_PASS, :]
            nc.sync.dma_start(out=raw[:], in_=rows.rearrange("(a p j) r -> p a (j r)", p=P, j=PACK))
            down_raw[a] = raw[:, 0, :]

        def load_w4(first, last):
            part = held([P, PASSES, 2 * P * (last - first)], U8, "w4_%d" % first)
            words = w4_words[:, :, 2 * P * first : 2 * P * last].bitcast(I32).rearrange("a p n -> p a n")
            nc.sync.dma_start(out=part[:].bitcast(I32), in_=words)
            for c in range(first, last):
                w4[c] = part[:, :, 2 * P * (c - first) : 2 * P * (c + 1 - first)]

        buffer_of = {0: "table0", 1: "down_raw0", 2: "down_raw1", LAST_TILE: "table1"}

        def load_residual(c):
            raw = held([P, 1, T], F32, buffer_of.get(c, "residual%d" % c))
            nc.sync.dma_start(out=raw[:], in_=rT[c * P : (c + 1) * P, :].rearrange("(c p) t -> p c t", p=P))
            residual[c] = raw[:, 0, :]

        load_table(0, 0, TABLE_HEAD)
        load_table_scales()
        load_table(0, TABLE_HEAD, T)
        nc.sync.dma_start(out=b_rows[0:ROW_TILES, :], in_=b.rearrange("(c p) -> c p", p=P))
        load_down(0)
        load_down(1)
        nc.vector.tensor_copy(picked_scale[:], tab_scale[:].bitcast(U8).indirect(offsets[:]))
        load_table(1)
        place_table_scales()
        load_down(2)
        load_table(2)
        nc.sync.dma_start(out=up_raw[:], in_=up.rearrange("(p j) n -> p j n", j=PACK))
        load_w4_scales()
        load_w4(0, W4_FIRST_TILES)

        bias_bank = psum.tile([P, P], F32, name="bank")
        nc.tensor.transpose(bias_bank[:], b_rows[:], identity[:])
        bias = held([P, ROW_TILES], F32, "bias")
        nc.scalar.activation(out=bias[:], in_=bias_bank[:, 0:ROW_TILES], func=IDENTITY)

        v_words = [held([P, S], U32, "v_words%d" % a) for a in range(PASSES)]
        down_words = held([P, PASSES, R], U32, "down_words")
        down_scale = held([P, PASSES, R], U8, "down_scale")

        def gather_words(a, cols):
            nc.vector.tensor_copy(v_words[a][:, cols], table[a][:].bitcast(U32).indirect(list_part(cols)))

        def quantize_down(a):
            down_bf = held([P, PACK * R], BF16, "down_bf%d" % a)
            rounded = down_bf[:].rearrange("p (t m j) -> p m j t", t=PACK, j=PACK)
            raw = down_raw[a].rearrange("p (j m t) -> p m j t", j=PACK, t=PACK)
            if a == PASSES - 1:
                nc.scalar.copy(out=rounded[:, :, :, 0:2], in_=raw[:, :, :, 0:2])
                nc.vector.tensor_copy(out=rounded[:, :, :, 2:4], in_=raw[:, :, :, 2:4])
            else:
                nc.scalar.copy(out=rounded, in_=raw)
            nc.vector.quantize_mx(out=down_words[:, a, :].bitcast(FP8X4), scales=down_scale[:, a, :], in_=down_bf[:])

        gather_words(0, slice(0, S))
        quantize_down(0)
        quantize_down(1)
        gather_words(1, slice(0, S))
        quantize_down(2)
        for j in range(0, S, QUARTER):
            gather_words(PASSES - 1, slice(j, j + QUARTER))

        load_residual(0)
        load_w4(W4_FIRST_TILES, W4_HEAD_TILES)
        for c in range(1, TILES_AHEAD_OF_W4_REST):
            load_residual(c)
        load_w4(W4_HEAD_TILES, ROW_TILES)
        for c in range(TILES_AHEAD_OF_W4_REST, ROW_TILES):
            load_residual(c)

        groups = WHOLE_STORES + tuple((c,) for c in range(WHOLE_STORES[-1][-1] + 1, ROW_TILES))
        group_tile = {tiles: held([P, len(tiles), S], F32, "result%d" % tiles[0]) for tiles in groups}
        result = {c: group_tile[tiles][:, c - tiles[0], :] for tiles in groups for c in tiles}
        up_words = held([P, M], U32, "up_words")
        up_scale = held([P, M], U8, "up_scale")

        def quantize_up(half):
            up_bf = held([P, PACK * BANK], BF16, "up_bf%d" % half)
            round_copy = nc.vector.tensor_copy if half == 0 else nc.scalar.copy
            first = half * BANK
            for n in range(0, BANK, UP_PIECE):
                round_copy(
                    out=up_bf[:, PACK * n : PACK * (n + UP_PIECE)].rearrange("p (c i j) -> p c j i", i=4, j=PACK),
                    in_=up_raw[:, :, first + n : first + n + UP_PIECE].rearrange("p j (c i) -> p c j i", i=4),
                )
            step = UP_PIECE if half == 0 else BANK
            for n in range(0, BANK, step):
                cols = slice(first + n, first + n + step)
                nc.vector.quantize_mx(
                    out=up_words[:, cols].bitcast(FP8X4),
                    scales=up_scale[:, cols],
                    in_=up_bf[:, PACK * n : PACK * (n + step)],
                )

        h_words = held([P, S], U32, "h_words")
        h_scale = held([P, S], U8, "h_scale")
        h_bf = [held([P, PACK * BANK], BF16, "h_bf%d" % half) for half in range(HALVES)]
        h_banks = [psum.tile([P, PACK, H_COLS], F32, name="bank") for i in range(S // H_COLS)]
        for a in range(PASSES):
            for i, h_bank in enumerate(h_banks):
                cols = slice(i * H_COLS, (i + 1) * H_COLS)
                for t in range(PACK):
                    nc.tensor.matmul_mx(
                        out=h_bank[:, t, :],
                        lhsT=down_words[:, a, t * P : (t + 1) * P].bitcast(FP8X4),
                        lhsT_scale=down_scale[:, a, t * P : (t + 1) * P],
                        rhs=v_words[a][:, cols].bitcast(FP8X4),
                        rhs_scale=v_scale[:, a, :].bitcast(U8)[:, cols],
                        start=(a == 0 and t == 0),
                        stop=(a == PASSES - 1 and t == PACK - 1),
                    )
        for i, h_bank in enumerate(h_banks):
            half, part = divmod(i, PACK)
            round_copy = nc.vector.tensor_copy if i in H_BANKS_ON_VECTOR else nc.scalar.copy
            round_copy(
                out=h_bf[half][:, part * BANK : (part + 1) * BANK].rearrange("p (n t) -> p n t", t=PACK),
                in_=h_bank[:].rearrange("p t n -> p n t"),
            )
        for half in range(HALVES):
            cols = slice(half * BANK, (half + 1) * BANK)
            nc.vector.quantize_mx(out=h_words[:, cols].bitcast(FP8X4), scales=h_scale[:, cols], in_=h_bf[half][:])
        for half in range(HALVES):
            quantize_up(half)

        def sum_y(c, cols):
            rows = slice(c * P, (c + 1) * P)
            y_bank = psum.tile([P, BANK], F32, name="bank")
            for a in range(PASSES):
                nc.tensor.matmul_mx(
                    out=y_bank[:],
                    lhsT=w4[c][:, a, :].bitcast(FP4X4),
                    lhsT_scale=w4_scale[:, a, :].bitcast(U8)[:, rows],
                    rhs=v_words[a][:, cols].bitcast(FP8X4),
                    rhs_scale=v_scale[:, a, :].bitcast(U8)[:, cols],
                    start=(a == 0),
                    stop=False,
                )
            nc.tensor.matmul_mx(
                out=y_bank[:],
                lhsT=up_words[:, rows].bitcast(FP8X4),
                lhsT_scale=up_scale[:, rows],
                rhs=h_words[:, cols].bitcast(FP8X4),
                rhs_scale=h_scale[:, cols],
                start=False,
                stop=True,
            )
            return y_bank

        def gather_residual(into, c, cols):
            nc.vector.tensor_copy(into, residual[c].indirect(list_part(cols)))

        halves = [slice(half * BANK, (half + 1) * BANK) for half in range(HALVES)]
        group_ending_at = {tiles[-1]: tiles for tiles in WHOLE_STORES}
        for c in range(ROW_TILES):
            rows = slice(c * P, (c + 1) * P)
            for cols in halves:
                gather_residual(result[c][:, cols], c, cols)
            y_biased = staged.tile([P, S], F32, name="y_biased", align_bytes=ALIGN)
            for cols in halves:
                y_bank = sum_y(c, cols)
                split = cols.stop if c < LAST_TILE else max(cols.start, QUARTER)
                if split > cols.start:
                    part = slice(cols.start, split)
                    nc.scalar.activation(
                        out=y_biased[:, part],
                        in_=y_bank[:, 0 : split - cols.start],
                        func=IDENTITY,
                        bias=bias[:, c : c + 1],
                    )
                    nc.gpsimd.tensor_tensor(
                        out=result[c][:, part], in0=y_biased[:, part], in1=result[c][:, part], op=ADD
                    )
                for j in range(split, cols.stop, QUARTER):
                    part = slice(j, j + QUARTER)
                    nc.vector.scalar_tensor_tensor(
                        out=result[c][:, part],
                        in0=y_bank[:, j - cols.start : j - cols.start + QUARTER],
                        scalar=bias[:, c : c + 1],
                        in1=result[c][:, part],
                        op0=ADD,
                        op1=ADD,
                    )
                    if split == cols.start:
                        nc.sync.dma_start(out=out[rows, part], in_=result[c][:, part])
                if c > WHOLE_STORES[-1][-1] and split > cols.start:
                    nc.sync.dma_start(out=out[rows, cols], in_=result[c][:, cols])
            if c in group_ending_at:
                tiles = group_ending_at[c]
                written = out[tiles[0] * P : (c + 1) * P, :]
                nc.sync.dma_start(out=written.rearrange("(c p) j -> p c j", p=P), in_=group_tile[tiles][:])
